import numpy as np, ml_dtypes
CORES = [36,164,52,180,100,228,116,244]
N = 8
BF = ml_dtypes.bfloat16
def gentries(a):
    return np.ascontiguousarray(a.reshape(8, 16, -1).transpose(0, 2, 1)).reshape(8, -1)
def gtable(e):
    e = np.asarray(e); return np.ascontiguousarray(e.reshape(8, -1, 16).transpose(0, 2, 1)).reshape(128, -1).astype(np.int32)
V, M, J, T, S, H = 2048, 64, 4, 3, 3, 12
L = J * M
def base(rng):
    c = np.arange(V)
    lv = rng.integers(0, 64, (N, 8, 1, V)); lv[:, 1::2] = (c * 127) // V
    x = lv + rng.integers(0, 128, (N, 8, 16, V))
    k = rng.integers(0, V, (N, 8, 16, V)); k[:, 1::2] = (c + rng.integers(-(V // 32), V // 8, (N, 4, 16, V))) & (V - 1)
    z = rng.integers(20, 200, (N, 8, 1, T, M)) + rng.integers(0, 56, (N, 8, 16, T, M))
    return x, k, z, rng.integers(0, V, (N, 8, T, J, M))
def pack(x, k, z, v):
    return {"x0": np.ascontiguousarray(x.reshape(N, 128, V)).astype(np.float32).astype(BF), "k0": np.ascontiguousarray(k.reshape(N, 128, V)).astype(np.int32),
            "z0": np.ascontiguousarray(z.reshape(N, 128, T * M)).astype(np.float32).astype(BF), "v0": np.stack([gtable(a.reshape(8, -1)) for a in v])}
def setup_inputs(rng):
    return pack(*base(rng))
def setup_inputs_spread(rng):
    x = (np.exp2(8 * rng.random((N, 8, 1, V))) * rng.random((N, 8, 16, V))).astype(np.int64)
    z = (np.exp2(8 * rng.random((N, 8, 1, T, M))) * rng.random((N, 8, 16, T, M))).astype(np.int64)
    return pack(x, (V * rng.random((N, 8, 16, V)) ** 2).astype(np.int64), z, (V * rng.random((N, 8, T, J, M)) ** 3).astype(np.int64))
def setup_inputs_ends(rng):
    def tips(hi, *shape):
        return hi * rng.integers(0, 2, shape)
    h = rng.random((N, 8, 1, V)); x = np.where(h < 0.25, 255, np.where(h < 0.5, 0, tips(255, N, 8, 16, V)))
    k = np.where(rng.random((N, 8, 16, V)) < 0.8, tips(V - 1, N, 8, 16, V), rng.integers(8, V - 1, (N, 8, 16, V)))
    h = rng.random((N, 8, 1, T, M)); z = np.where(h < 0.3, 0, np.where(h < 0.6, 255, 255 * (rng.random((N, 8, 16, T, M)) < 0.25)))
    v = np.where(rng.random((N, 8, T, J, M)) < 0.7, tips(V - 1, N, 8, T, J, M), rng.integers(8, V - 1, (N, 8, T, J, M)))
    even = ((np.arange(N)[:, None] + np.arange(8)[None, :] + N) & 1 == 0)[:, :, None]
    x[..., V - 1] = np.where(even, 255, x[..., V - 1]); x[..., 0] = np.where(even, x[..., 0], 255)
    i = np.arange(16); nl = H + 1 - (H & 1)
    z[:, :, :, 0, M - 1] = 0; z[:, :, :, 0, M - 2] = np.where(i < H, 254, 255); z[:, :, :, 0, M - 3] = np.where(i < nl, 254, 255)
    v[:, :, 0, :, M - 2:] = V - 1; k[:, :, 0, V - 1] = V - 1
    x[..., 565] = 255; k[:, :, 0, 2] = 565; k[:, :, 0, 3] = V - 1; v[:, :, 0, 0, M - 3] = 2; v[:, :, 0, 1, M - 3] = 3
    x[..., 7] = 255 - (np.argsort(rng.random((N, 8, 16)), axis=2) == 0).astype(np.int64)
    k[:, :, :15, 6] = 7; k[:, :, 15, 6] = np.where(even[:, :, 0], V - 1, 0); z[:, :, :, 0, M - 5] = 0; v[:, :, 0, :, M - 5] = 6
    return pack(x, k, z, v)
def setup_inputs_corners(rng):
    x, k, z, v = base(rng); o = rng.permutation(8); c = np.arange(V)
    x[:, o[0], 8:] = 0
    x[:, o[1]] = rng.integers(1, 101, (N, 16, V)); z[:, o[1]] = 0; h = int(rng.integers(0, N))
    x[np.array([h, (h - J) % N]), o[1]] = rng.integers(200, 256, (2, 16, V)); z[:, o[1], :, 1:] = rng.integers(100, 150, (N, 16, T - 1, M))
    k[:, o[2]] = c
    k[:, o[3]] = (c + 1) & (V - 1); x[:, o[3]] = np.where(c % (S + 1) == 0, rng.integers(200, 256, (N, 16, V)), 0); z[:, o[3]] = rng.integers(100, 151, (N, 16, T, M))
    d = rng.integers(1, S + 2, (N, T, J, M))
    d[:, 0, :, 0] = S + 1; d[:, 0, :, 1] = S; d[:, 0, 0, 2] = S; d[:, 0, 1:, 2] = S + 1; d[:, 0, :-1, 3] = S; d[:, 0, -1, 3] = 1
    v[:, o[3]] = (rng.integers(0, V // (S + 1) - 1, (N, T, J, M)) + 1) * (S + 1) - d; v[:, o[3], 0, 0, 4] = V - 1
    x[:, o[4]] = 255 * (np.argsort(rng.random((N, 16, V)), axis=1) < H - 1 + (c & 3)); k[:, o[4]] = (rng.integers(0, V, (N, 16, V)) & (V - 4)) | (c & 3); z[:, o[4]] = 100
    k[:, o[5]] = (V - 1) * rng.integers(0, 2, (N, 16, V)); v[:, o[5]] = (V - 1) * rng.integers(0, 2, (N, T, J, M))
    h = rng.integers(0, 5, (N, 16, V))
    k[:, o[6]] = np.where(h == 0, 0, np.where(h == 1, V - 1, np.where(h == 2, c, np.where(h == 3, (c + 1) & (V - 1), (c - 1) & (V - 1)))))
    v[:, o[6]] = rng.choice(np.array([0, 1, V - 2, V - 1]), (N, T, J, M))
    v[:, o[7]] = rng.integers(0, V, (T, 1, 1))
    return pack(x, k, z, v)
def setup_inputs_ties(rng):
    x, k, z, v = base(rng)
    x = rng.integers(100, 103, x.shape); z = rng.integers(100, 102, z.shape); z[..., ::8] = 102
    for q in range(N):
        for g in range(0, 8, 2):
            few = rng.permutation(V)[:64]; few[0] = V - 1; k[q, g] = few[rng.integers(0, 64, (16, V))]
    k[:, ::3, 8:] = k[:, ::3, :8]
    k[:, 7, 14:, 1::2] = V - 1; x[:, 7, :, V - 1] = 103
    return pack(x, k, z, v)
def setup_inputs_meets(rng):
    x, k, z, v = base(rng)
    for q in range(N):
        for g in range(8):
            n = 8 + 16 * g; few = rng.permutation(V)[:n]; few[0] = 0; few[1] = V - 1
            k[q, g][:, few] = few[rng.integers(0, n, (16, n))]
            for j in range(1, J + 1): v[(q - j) % N, g, :, j - 1] = few[rng.integers(0, n, (T, M))]
    return pack(x, k, z, v)
def check_inputs(d):
    bad = []
    for k, lo, hi in (("x0", 0, 255), ("k0", 0, V - 1), ("z0", 0, 255), ("v0", 0, V - 1)):
        a = np.asarray(d[k]).astype(np.float64)
        if not (np.min(a) >= lo and np.max(a) <= hi): bad.append("range of " + k)
        elif np.any(a != np.floor(a)): bad.append("whole numbers of " + k)
    return bad
def to_hosts(a):
    return np.stack([np.concatenate([a[(q - j) % N, :, j - 1] for j in range(1, J + 1)], axis=1) for q in range(N)])
def to_owners(a):
    return np.stack([np.stack([a[(r + j) % N, :, (j - 1) * M:j * M] for j in range(1, J + 1)], axis=1) for r in range(N)])
def lowest(n, on):
    a = np.flatnonzero(on)
    return a[np.unique(n[a], return_index=True)[1]]
def reference(x0, k0, z0, v0):
    X = x0.astype(np.float32).astype(np.int64).reshape(N, 8, 16, V); K = k0.astype(np.int64).reshape(N, 8, 16, V)
    Z = z0.astype(np.float32).astype(np.int64).reshape(N, 8, 16, T, M); start = np.stack([gentries(a) for a in v0]).astype(np.int64).reshape(N, 8, T, J, M)
    odd = np.zeros(N, np.int64)
    for t in range(T):
        v = to_hosts(start[:, :, t])
        z = np.stack([np.concatenate([Z[(q - j) % N, :, :, t] for j in range(1, J + 1)], axis=2) for q in range(N)])
        b = np.full((N, 8, L), S + 1, np.int64); zb = np.zeros((N, 8, 16, L), np.int64); wb = np.zeros((N, 8, L), np.int64)
        logv, logk = [], []
        for s in range(1, S + 1):
            kv = np.take_along_axis(K, v[:, :, None, :], 3)
            ix = kv.transpose(0, 1, 3, 2).reshape(N, 8, L * 16)
            xk = np.take_along_axis(X, ix[:, :, None, :], 3).reshape(N, 8, 16, L, 16)
            score = np.add.reduce(np.maximum(xk - z[..., None], 0), axis=2)
            k = np.argmax(score, axis=-1)
            w = np.take_along_axis(kv, k[:, :, None, :], 2)[:, :, 0]
            xw = np.take_along_axis(X, w[:, :, None, :], 3)
            bid = np.add.reduce((xw > z).astype(np.int64), axis=2) >= H + odd[:, None, None]
            z = (z + xw) >> 1
            now = bid & (b > S)
            b = np.where(now, s, b); wb = np.where(now, w, wb); zb = np.where(now[:, :, None, :], z, zb)
            logv.append(v); logk.append(k); v = w
        u = (wb * np.add.reduce(zb, axis=2)) & (V - 1)
        bo = to_owners(b); win = np.argmin(bo, axis=2); first = np.min(bo, axis=2)
        uo = np.take_along_axis(to_owners(u), win[:, :, None, :], 2)
        every = np.zeros((N, 8, J, M), np.int64)
        end = to_hosts(every + first[:, :, None, :]); uw = to_hosts(every + uo)
        won = to_hosts(win[:, :, None, :] == np.arange(J)[None, None, :, None]) & (end <= S); lost = ~won & (end <= S)
        for q in range(N):
            for g in range(8):
                a = lowest(wb[q, g], won[q, g]); n = wb[q, g, a]
                X[q, g][:, n] = (X[q, g][:, n] + zb[q, g][:, a]) >> 1
                for s in range(S, 0, -1):
                    a = lowest(logv[s - 1][q, g], lost[q, g] & (end[q, g] >= s))
                    n = logv[s - 1][q, g, a]; i = logk[s - 1][q, g, a]; c = K[q, g, i, n]
                    K[q, g, i, n] = (((uw[q, g, a] * c) >> 5) + c + s) & (V - 1)
        odd = np.add.reduce(won.reshape(N, -1).astype(np.int64), axis=1) & 1
    f8 = np.arange(1, 9)[None, None, :, None]
    return {"yx": np.add.reduce(X.reshape(N, 128, 8, V // 8) * f8, axis=2).astype(np.float32), "yk": np.add.reduce(K.reshape(N, 128, 8, V // 8) * f8, axis=2).astype(np.float32)}

@@ -1,0 +1,512 @@
+from concourse.bass import DstId, RemoteDMATransfer
+from concourse.mybir import AluOpType as A, AxisListType, ActivationFunctionType as F
+
+f32, b16, h16, i32, u16 = "float32", "bfloat16", "float16", "int32", "uint16"
+SCRATCH = {}
+
+
+def _sb(dtype, **shapes):
+    for name, shape in shapes.items():
+        SCRATCH[name] = ("sbuf", [128] + (list(shape) if isinstance(shape, (list, tuple)) else [shape]), dtype)
+
+
+_sb(b16, X=2304, z0s=192, zc=768)
+_sb(f32, K=2304, VL=48)
+_sb(i32, K0=2048, v0s=48)
+_sb(h16, pk=240, ZL=960)
+_sb(u16, VLu=48, expo=16, offK=8)
+_sb(f32, it16=256, itb=256, gmask=8, pcol=1, dd=128, dmask=256, rst=128, keyc=(6, 8), zoffc=(6, 8), spare=16, thr=1, gm2=8, WIf=384)
+_sb(i32, pint=1, pr2=2)
+_sb(b16, I=128, nI=128, ones=128, Sel=8, order=128, chalf=256, tri=(16, 16), Pb=2048, Q8=2048, Is=384, WIb=1024, B1=128)
+_sb(h16, WIh=640)
+for _h in "01":
+    _sb(u16, **{"KvU" + _h: 128})
+    _sb(f32, **{"KvF" + _h: 128, "RC" + _h: 256, "ZM" + _h: 128})
+    _sb(b16, **{"XK" + _h: 2048, "XM" + _h: (16, 128), "St" + _h: 128, "xw" + _h: 128})
+    _sb(h16, **{"PA" + _h: 128})
+_sb(b16, OAs=768, ZB=1536)
+_sb(u16, WU=48)
+_sb(f32, wlf=(6, 8), CLS=(6, 16))
+_sb(h16, VR0=256, VR1=256, VR2=256, VR3=256, tmp=256)
+_sb(f32, bk=(6, 8), wpos=16, kz=(6, 8), kz2=(2, 8), zo=(2, 8), Wf=16, c23=32, eqw=16, pr=1, ZM2=256)
+_sb(i32, us=(6, 8), ui=(6, 8), ks=(6, 8), kb=(6, 8), m1=(2, 8), kw=(6, 8), kw1=(6, 8), kw2=(2, 8), kw3=(2, 8), Wi=(2, 8), uI=16)
+_sb(i32, RK0=(7, 16), RK1=(7, 16), RK2=(7, 16), n1=(4, 4), n2=(4, 4), best=(4, 4))
+_sb(u16, zou=16, Wu=16)
+_sb(b16, E0=(16, 256), E1=(16, 256), E2=(16, 256), E3=(16, 256), ON=64, onR=512, Zb=256, XWb=256, nX=256)
+_sb(f32, Um=(4, 256), Am=(4, 256), pp=(4, 256), ns=64, nd=64, of=64)
+_sb(i32, qq=(4, 256), rr=(4, 256))
+_sb(b16, cD=1024)
+_sb(u16, ou=64)
+_sb(f32, oX=256, oK=256)
+_sb(h16, KH=1280)
+for _n in ("D0", "D1", "D2", "D3"):
+    SCRATCH[_n] = ("psum", [128, 8, 64], f32)
+for _n in ("SC", "OA", "WL", "ZD"):
+    SCRATCH[_n] = ("psum", [128, 512], f32)
+
+_LOADS = ["lz", "lv", "lx", "lk0", "lk1", "lk2", "lk3", "sx", "sk"]
+SEMAPHORES = ["qv", "qs", "qt", "qg", "zarr", "karr0", "karr1", "karr2", "sent"] + _LOADS
+FILL = (0, 3, 2, 0)
+BIG = 8388608.0
+
+
+def rank_program(g, core, T, topo):
+    rank = T.rank_of(core)
+    if rank is None:
+        return
+    n = len(T.cores)
+    Q = {"v": g.vector, "s": g.scalar, "t": g.tensor, "g": g, "y": g.sync}
+    V, S, P = Q["v"], Q["s"], Q["t"]
+    cnt, snap, wr, rd = {}, {}, {}, {}
+    know = {q: {} for q in Q}
+
+    def deps(q, R, W):
+        own, d = "q" + q, {}
+
+        def want(table, t, same):
+            for sem, val in table.get(t, {}).items():
+                if same or sem != own:
+                    d[sem] = max(d.get(sem, 0), val)
+        for t in R:
+            want(wr, t, True)
+            if t[0] == "#":
+                want(rd, t, False)
+        for t in W:
+            want(wr, t, False)
+            want(rd, t, False)
+        for sem in sorted(d, key=lambda x: (x == own, x)):
+            val, k = d[sem], know[q]
+            if k.get(sem, 0) >= val:
+                continue
+            Q[q].wait_ge(T.sem[sem], val)
+            for s2, v2 in snap.get((sem, val), {}).items():
+                k[s2] = max(k.get(s2, 0), v2)
+            k[sem] = val
+
+    def done(q, sem, inc, R, W):
+        cnt[sem] = cnt.get(sem, 0) + inc
+        snap[(sem, cnt[sem])] = dict(know[q])
+        for t in R:
+            rd.setdefault(t, {})[sem] = cnt[sem]
+        for t in W:
+            wr.setdefault(t, {})[sem] = cnt[sem]
+
+    def op(q, R, W, f, *a, **k):
+        R, W = R.split(), W.split()
+        deps(q, R, W)
+        f(*a, **k).then_inc(T.sem["q" + q], 1)
+        done(q, "q" + q, 1, R, W)
+
+    def mm(R, W, calls):
+        R, W = R.split(), W.split()
+        deps("t", R, W)
+        for c in calls[:-1]:
+            P.matmul(*c)
+        P.matmul(*calls[-1]).then_inc(T.sem.qt, 1)
+        done("t", "qt", 1, R, W)
+
+    def dma(q, sem, R, W, out, in_):
+        R, W = R.split(), W.split()
+        deps(q, R, W)
+        Q[q].dma_start(out, in_).then_inc(T.sem[sem], 16)
+        done(q, sem, 16, R, W)
+
+    def send(R, sem, src, dsts):
+        deps("g", R.split(), [])
+        ids, mask = [], topo.mask(core, T.cores[dsts[0][0]])
+        for r, _ in dsts:
+            rid, pid = topo.addr(T.cores[r], core)
+            ids.append(DstId(rid=rid, pnc=pid))
+            mask &= topo.mask(core, T.cores[r])
+        g.remote_dma_fused([RemoteDMATransfer(dst_ids=ids, dma_engine_mask=mask, remote_sem=T.sem[sem], srcs=[src],
+                                              dsts=[p for _, p in dsts])], local_sem=T.sem.sent)
+        e = bin(mask).count("1")
+        cnt["sent"] = cnt.get("sent", 0) + e
+        return e * len(dsts)
+
+    def arrives(tag, sem, val):
+        cnt[sem] = val
+        wr.setdefault(tag, {})[sem] = val
+
+    ts, tt, cp, act = V.tensor_scalar, V.tensor_tensor, V.tensor_copy, S.activation
+
+    dma("y", "lz", "", "z0s", T.z0s[:], T.z0[:])
+    dma("y", "lv", "", "v0s", T.v0s[:], T.v0[:])
+    for b in range(4):
+        dma("y", "lk%d" % b, "", "K0%d" % b, T.K0[:, 512 * b:512 * b + 512], T.k0[:, 512 * b:512 * b + 512])
+    dma("s", "lx", "", "X", T.X[:, 0:2048], T.x0[:])
+
+    def iota(buf, pattern, base, cm):
+        op("g", "", buf, g.iota, T[buf][:], pattern, base, cm, allow_small_or_imprecise_dtypes=True)
+    iota("dd", [[-1, 128]], 0, 1)
+    iota("gm2", [[-16, 8]], 0, 1)
+    iota("pint", [[0, 1]], 0, 1)
+    op("v", "z0s", "pk", cp, T.pk[:, 0:192], T.z0s[:])
+    op("v", "v0s", "pk", cp, T.pk[:, 192:240], T.v0s[:])
+    got = send("pk", "zarr", T.pk[:], [((rank + j) % n, T.ZL[:, 240 * (j - 1):240 * j]) for j in (1, 2, 3, 4)])
+    arrives("ZL", "zarr", got)
+
+    iota("it16", [[0, 16], [1, 16]], 0, 0)
+    iota("rst", [[0, 8], [1, 16]], 0, 0)
+    iota("order", [[0, 8], [-1, 16]], 15, 0)
+    iota("itb", [[16, 16], [0, 16]], 0, 0)
+    iota("keyc", [[8192, 3], [-2048, 4], [0, 4]], 4 * 2048, 0)
+    iota("zoffc", [[512, 3], [256, 2], [16, 8]], 128, 0)
+    iota("spare", [[16, 16]], 2048, 0)
+    op("v", "dd", "I", ts, T.I[:], T.dd[:], 0.0, None, A.is_equal)
+    op("v", "dd", "nI", ts, T.nI[:], T.dd[:], 0.0, -1.0, A.is_equal, A.mult)
+    op("v", "gm2", "pc", ts, T.gmask[:], T.gm2[:], 0.0, None, A.is_ge)
+    op("v", "gm2", "gm2", ts, T.gm2[:], T.gm2[:], 16.0, None, A.is_lt)
+    op("v", "gm2 pc", "gmask", tt, T.gmask[:], T.gmask[:], T.gm2[:], A.mult)
+    op("v", "pint", "pint", ts, T.pint[:], T.pint[:], 15, None, A.bitwise_and)
+    op("v", "pint", "pcol", cp, T.pcol[:], T.pint[:])
+    op("v", "gmask", "Sel", ts, T.Sel[:], T.gmask[:], 16.0, None, A.mult)
+    op("v", "", "ones", V.memset, T.ones[:], 1.0)
+    op("v", "", "chalf", V.memset, T.chalf[:], -0.5)
+    op("v", "", "thr", V.memset, T.thr[:], 8.0)
+    op("v", "", "Pb", V.memset, T.Pb[:], 0.0)
+    op("v", "", "B1", V.memset, T.B1[:], 0.0)
+    op("v", "it16 pcol", "dmask", ts, T.dmask[:], T.it16[:], T.pcol[:], None, A.is_equal)
+    op("v", "it16 pcol", "tri", ts, T.tri[:], T.it16[:], T.pcol[:], None, A.is_gt)
+    op("v", "rst", "rst", ts, T.rst[:], T.rst[:], 0.0, None, A.is_gt)
+    op("v", "it16", "expo", cp, T.expo[:], T.it16[:, 0:16])
+    op("v", "itb", "offK", ts, T.offK[:], T.itb[:, 0:128:16], 15.0, None, A.add)
+    op("v", "zoffc pcol", "zoffc", ts, T.zoffc[:], T.zoffc[:], T.pcol[:], None, A.add)
+    op("v", "spare pcol", "spare", ts, T.spare[:], T.spare[:], T.pcol[:], None, A.add)
+    for p in range(16):
+        op("s", "gmask", "B1", act, T.B1[:, p:128:16], T.gmask[:], F.Copy)
+        op("s", "gmask", "Pb", act, T.Pb[:, 128 * p + p:128 * (p + 1):16], T.gmask[:], F.Copy)
+
+    for b in range(4):
+        op("v", "K0%d" % b, "K", cp, T.K[:, 512 * b:512 * b + 512], T.K0[:, 512 * b:512 * b + 512])
+
+    def starts(t):
+        for j in range(4):
+            op("v", "ZL", "zc%d" % t, cp, T.zc[:, 256 * t + 64 * j:256 * t + 64 * j + 64], T.ZL[:, 240 * j + 64 * t:240 * j + 64 * t + 64])
+            c = 16 * t + 4 * j
+            op("v", "ZL", "VL%d" % t, cp, T.VL[:, c:c + 4], T.ZL[:, 240 * j + 192 + c:240 * j + 192 + c + 4])
+        op("v", "VL%d" % t, "VLu%d" % t, cp, T.VLu[:, 16 * t:16 * t + 16], T.VL[:, 16 * t:16 * t + 16])
+    starts(0)
+
+    late = [("v", "", "Q8", V.memset, T.Q8[0:8, :], 1.0),
+            ("g", "Q8", "Q8", g.affine_select, T.Q8[0:8, :], T.Q8[0:8, :], [[-1, 16], [1, 128]], A.is_equal, 0.0, 0, -16)]
+    for s in (1, 2, 3):
+        late.append(("s", "I", "Is", act, T.Is[:, 128 * s - 128:128 * s], T.I[:], F.Copy, 0.0, 32.0 * s))
+    for a in range(8):
+        late.append(("s", "I", "WIb", act, T.WIb[:, 128 * a:128 * a + 128], T.I[:], F.Copy, 0.0, a + 1.0))
+        if a < 5:
+            late.append(("v", "I", "WIh", ts, T.WIh[:, 128 * a:128 * a + 128], T.I[:], a + 1.0, None, A.mult))
+        else:
+            late.append(("s", "I", "WIf", act, T.WIf[:, 128 * (a - 5):128 * (a - 4)], T.I[:], F.Copy, 0.0, a + 1.0))
+
+    Kwin, Xwin = T.K[:, 0:2048], T.X[:, 0:2048]
+
+    def slot(s, h):
+        return ((2 - s) * 2 + h) * 256
+
+    def zat(t, s, h):
+        return ("zc%d" % t, T.zc, 256 * t + 128 * h) if s == 0 else ("z%d%d" % (s - 1, h), T.ZB, slot(s - 1, h) + 128)
+
+    def holders(t, s, h, w):
+        return ("VLu%d" % t, T.VLu[:, 16 * t + 8 * h:16 * t + 8 * h + w]) if s == 0 else \
+            ("WU%d%d" % (s - 1, h), T.WU[:, 16 * (s - 1) + 8 * h:16 * (s - 1) + 8 * h + w])
+
+    def zpath1(t, s, h):
+        H = str(h)
+        tag, zb, z0 = zat(t, s, h)
+        zz = zb[:, z0:z0 + 128]
+        w = "WU%d%d" % (s, h)
+        op("s", "X " + w, "xw" + H, act, T["xw" + H][:], Xwin.indirect(T.WU[:, 16 * s + 8 * h:16 * s + 8 * h + 8]), F.Copy)
+        xw = T["xw" + H][:]
+        mm("I nI chalf xw%s %s" % (H, tag), "#ZD", [
+            (T.ZD[:, 0:256], T.I[:], T.chalf[:], True, False), (T.ZD[:, 0:128], T.I[:], xw, False, False),
+            (T.ZD[:, 128:256], T.I[:], xw, False, False), (T.ZD[:, 0:128], T.nI[:], zz, False, False),
+            (T.ZD[:, 128:256], T.I[:], zz, False, True)])
+
+    def zpath2(t, s, h):
+        H = str(h)
+        op("s", "#ZD", "ZM" + H, act, T["ZM" + H][:], T.ZD[:, 128:256], F.Identity, BIG, 0.5)
+        o = slot(s, h)
+        op("s", "ZM" + H, "z%d%d" % (s, h), act, T.ZB[:, o + 128:o + 256], T["ZM" + H][:], F.Identity, -BIG)
+
+    def zpath3(t, s, h):
+        o = slot(s, h)
+        op("s", "#ZD", "sg%d%d" % (s, h), act, T.ZB[:, o:o + 128], T.ZD[:, 0:128], F.Sign)
+
+    def sums(steps):
+        tags = " ".join("z%d%d sg%d%d" % (s, h, s, h) for s in steps for h in (0, 1))
+        a, b = slot(max(steps), 0), slot(min(steps), 1) + 256
+        w = (b - a) // 16
+        mm("Pb " + tags, "#ZD", [
+            (T.ZD[:, 256:256 + w], T.Pb[:, 128 * p:128 * p + 128], T.ZB[:, a + p:b:16], p == 0, p == 15) for p in range(16)])
+        op("s", "#ZD", "CLS%d" % len(steps), act, T.CLS[:, a // 256:b // 256, :], T.ZD[:, 256:256 + w], F.Copy)
+
+    def sub(t, s, h, b):
+        H, ch, kh = str(h), b // 2, b % 2
+        tag, zb, z0 = zat(t, s, h)
+        zz = zb[:, z0 + 64 * ch:z0 + 64 * ch + 64]
+        D = T["D%d" % (2 * ch + kh)]
+        calls = []
+        for k8 in range(8):
+            k = 8 * kh + k8
+            calls.append((D[:, k8, :], T.I[:], T["XK" + H][:, 1024 * ch + k:1024 * (ch + 1):16], True, False))
+            calls.append((D[:, k8, :], T.nI[:], zz, False, True))
+        mm("I nI XK%s%d %s" % (H, ch, tag), "#D%d" % (2 * ch + kh), calls)
+
+    def relu(h, b):
+        H, ch, kh = str(h), b // 2, b % 2
+        out = T["XM" + H][:, 8 * kh:8 * kh + 8, 64 * ch:64 * ch + 64]
+        if ch == 0:
+            op("v", "#D%d" % b, "XM%s%d" % (H, b), ts, out, T["D%d" % b][:], 0.0, None, A.max)
+        else:
+            op("s", "#D%d" % b, "XM%s%d" % (H, b), act, out, T["D%d" % b][:], F.Relu)
+
+    def kvf(t, s, h):
+        tag, lst = holders(t, s, h, 8)
+        op("s", "K " + tag, "KvF%d" % h, act, T["KvF%d" % h][:], Kwin.indirect(lst), F.Copy)
+
+    def period(t, front, tail, fill):
+        if front:
+            s, h = front
+            H = str(h)
+            tag, lst = holders(t, s, h, 8)
+            op("v", "K " + tag, "KvU" + H, cp, T["KvU" + H][:], Kwin.indirect(lst))
+        if tail:
+            s2, h2 = tail
+            G = str(h2)
+            mm("ones order Sel " + " ".join("XM%s%d" % (G, b) for b in range(4)), "#SC",
+               [(T.SC[:, 0:128], T.ones[0:1, :], T.order[0:1, :], True, False)] +
+               [(T.SC[:, k:128:16], T["XM" + G][:, k, :], T.Sel[:], False, k == 15) for k in range(16)])
+        if front:
+            if s:
+                zpath2(t, s - 1, h)
+            op("v", "X KvU" + H, "XK%s0" % H, cp, T["XK" + H][:, 0:1024], Xwin.indirect(T["KvU" + H][:, 0:64]))
+            op("s", "X KvU" + H, "XK%s1" % H, act, T["XK" + H][:, 1024:2048], Xwin.indirect(T["KvU" + H][:, 64:128]), F.Copy)
+            if s:
+                zpath3(t, s - 1, h)
+            kvf(t, s, h)
+            sub(t, s, h, 0)
+        else:
+            zpath2(t, s2, 0)
+            zpath3(t, s2, 0)
+        if tail:
+            op("v", "rst #SC", "R" + G, V.tensor_tensor_scan, T["RC" + G][:, 0:128], T.rst[:], T.SC[:, 0:128], 0.0, A.mult, A.max)
+            op("v", "#SC", "C" + G, cp, T["RC" + G][:, 128:256], T.SC[:, 0:128])
+            op("v", "offK R%s C%s" % (G, G), "St" + G, tt, T["St" + G][:], T["RC" + G][:, 0:128].indirect(T.offK[:]),
+               T["RC" + G][:, 128:256], A.is_equal)
+            mm("I St" + G, "#OA", [(T.OA[:, 0:128], T["St" + G][:], T.I[:], True, True)])
+        fill(0)
+        if front:
+            sub(t, s, h, 1)
+            relu(h, 0)
+        fill(1)
+        if tail:
+            op("v", "#OA KvF" + G, "PA" + G, tt, T["PA" + G][:], T.OA[:, 0:128], T["KvF" + G][:], A.mult)
+            op("s", "#OA", "OAs%d" % s2, act, T.OAs[:, 256 * s2 + 128 * h2:256 * s2 + 128 * h2 + 128], T.OA[:, 0:128], F.Copy)
+            if front:
+                sub(t, s, h, 2)
+            mm("Pb PA" + G, "#WL", [
+                (T.WL[:, 0:8], T.Pb[:, 128 * p:128 * p + 128], T["PA" + G][:, p:128:16], p == 0, p == 15) for p in range(16)])
+            if s2 < 2:
+                vr = "VR%d" % (s2 + 2)
+                mm("B1 PA" + G, "#OA", [(T.OA[:, 128:256], T.B1[:], T["PA" + G][:], True, True)])
+        if front:
+            relu(h, 1)
+            if not tail:
+                sub(t, s, h, 2)
+            relu(h, 2)
+            sub(t, s, h, 3)
+        else:
+            sums((0, 1))
+        fill(2)
+        if tail:
+            op("v", "#WL", "WU%d%d" % (s2, h2), cp, T.WU[:, 16 * s2 + 8 * h2:16 * s2 + 8 * h2 + 8], T.WL[:, 0:8])
+            zpath1(t, s2, h2)
+            op("s", "#WL", "wl%d" % s2, act, T.wlf[:, 4 - 2 * s2 + h2, :], T.WL[:, 0:8], F.Copy)
+            if s2 < 2:
+                op("v", "#OA", vr, cp, T[vr][:, 128 * h2:128 * h2 + 128], T.OA[:, 128:256])
+        if front:
+            relu(h, 3)
+        fill(3)
+
+    def spread(tag, lst):
+        op("v", "dmask expo " + tag, "tmp", tt, T.tmp[:], lst.indirect(T.expo[:]), T.dmask[:], A.mult)
+        mm("B1 tmp", "#OA", [(T.OA[:, 256:512], T.B1[:], T.tmp[:], True, True)])
+
+    def first(t):
+        spread("VL%d" % t, T.VL[:, 16 * t:16 * t + 16])
+        op("v", "#OA", "VR1", cp, T.VR1[:], T.OA[:, 256:512])
+
+    def equal(i, tag, col):
+        e = T["E%d" % i]
+        todo = [("v", "VR%d %s" % (i, tag), "E%d" % i, ts, e[:, c, 0:256 - 16 * c], T["VR%d" % i][:, 16 * c:256], col(c), None, A.is_equal)
+                for c in range(16)]
+        todo.append(("v", "tri E%d" % i, "E%d" % i, tt, e[:, :, 0:16], e[:, :, 0:16], T.tri[:], A.mult))
+        return todo
+
+    def race(t):
+        todo = []
+
+        def fill(k, lots=0):
+            for _ in range(min(len(todo), lots)):
+                op(*todo.pop(0))
+        some = lambda k: fill(k, FILL[k])
+        vlc = lambda c: T.VL[:, 16 * t + c:16 * t + c + 1]
+        wc = lambda s: (lambda c: T.wlf[:, 4 - 2 * s + c // 8, c % 8:c % 8 + 1])
+        period(t, (0, 0), None, lambda k: k == 0 and first(t))
+        todo += equal(1, "VL%d" % t, vlc)
+        if t == 0:
+            todo += late
+        period(t, (0, 1), (0, 0), some)
+        period(t, (1, 0), (0, 1), some)
+        todo += equal(2, "wl0", wc(0))
+        period(t, (1, 1), (1, 0), some)
+        period(t, (2, 0), (1, 1), some)
+        todo += equal(3, "wl1", wc(1))
+        period(t, (2, 1), (2, 0), some)
+        period(t, None, (2, 1), lambda k: fill(k, (0, 4, 6, 0)[k]))
+        zpath2(t, 2, 1)
+        zpath3(t, 2, 1)
+        sums((2,))
+        fill(0, 8)
+        cls = "CLS1 CLS2"
+        rk, RK = "RK%d" % t, T["RK%d" % t]
+        key = RK[:, 3, :]
+        op("v", "thr " + cls, "bk", ts, T.bk[:], T.CLS[:, :, 0:8], T.thr[:], None, A.is_ge)
+        op("v", "wl0 wl1 wl2 " + cls, "us", tt, T.us[:], T.wlf[:], T.CLS[:, :, 8:16], A.mult)
+        op("v", "us", "ui", ts, T.ui[:], T.us[:], 2047, None, A.bitwise_and)
+        op("v", "ui keyc", "ks", tt, T.ks[:], T.ui[:], T.keyc[:], A.add)
+        op("v", "ks bk", "kb", tt, T.kb[:], T.ks[:], T.bk[:], A.mult)
+        op("v", "kb", "m1", tt, T.m1[:], T.kb[:, 0:2, :], T.kb[:, 2:4, :], A.max)
+        op("v", "kb m1", "key%d" % t, tt, key, T.m1[:], T.kb[:, 4:6, :], A.max)
+        got = send("key%d" % t, "karr%d" % t, key, [((rank - d) % n, RK[:, 3 - d, :]) for d in (-3, -2, -1, 1, 2, 3)])
+        arrives(rk, "karr%d" % t, got)
+        op("v", "key%d" % t, "wpos", ts, T.wpos[:], key, 0.5, None, A.is_ge)
+        op("v", "bk zoffc", "kz", tt, T.kz[:], T.zoffc[:], T.bk[:], A.mult)
+        op("v", "keyc wl0 wl1 wl2", "kw", tt, T.kw[:], T.wlf[:], T.keyc[:], A.add)
+        op("v", "kz", "kz2", tt, T.kz2[:], T.kz[:, 0:2, :], T.kz[:, 2:4, :], A.max)
+        op("v", "kw bk", "kw1", tt, T.kw1[:], T.kw[:], T.bk[:], A.mult)
+        op("v", "kz kz2", "zo", tt, T.zo[:], T.kz2[:], T.kz[:, 4:6, :], A.max)
+        op("v", "kw1", "kw2", tt, T.kw2[:], T.kw1[:, 0:2, :], T.kw1[:, 2:4, :], A.max)
+        op("v", "zo", "zou", cp, T.zou[:], T.zo[:])
+        op("v", "kw1 kw2", "kw3", tt, T.kw3[:], T.kw2[:], T.kw1[:, 4:6, :], A.max)
+        op("v", "kw3", "Wi", ts, T.Wi[:], T.kw3[:], 2047, None, A.bitwise_and)
+        op("v", "Wi", "Wf", cp, T.Wf[:], T.Wi[:])
+        op("v", "Wi", "Wu", cp, T.Wu[:], T.Wi[:])
+        spread("Wf", T.Wf[:])
+        zb = " ".join("z%d%d sg%d%d" % (s, h, s, h) for s in range(3) for h in range(2))
+        op("s", "zou " + zb, "Zb", act, T.Zb[:], T.ZB[:].indirect(T.zou[:]), F.Copy)
+        op("s", "X Wu", "XWb", act, T.XWb[:], Xwin.indirect(T.Wu[:]), F.Copy)
+        mm("I chalf Zb XWb", "#ZD", [(T.ZD[:, 0:256], T.I[:], T.chalf[:], True, False), (T.ZD[:, 0:256], T.I[:], T.Zb[:], False, False),
+                                     (T.ZD[:, 0:256], T.I[:], T.XWb[:], False, True)])
+        op("s", "#ZD", "ZM2", act, T.ZM2[:], T.ZD[:, 0:256], F.Identity, BIG, 0.5)
+        op("s", "ZM2", "nX", act, T.nX[:], T.ZM2[:], F.Identity, -BIG)
+        for s in (1, 2, 3):
+            mm("Is OAs%d" % (s - 1), "#D%d" % s, [(T["D%d" % s][:, 0:4, :], T.Is[:, 128 * s - 128:128 * s], T.OAs[:, 256 * s - 256:256 * s], True, True)])
+        fill(0, 99)
+        op("v", "#OA", "VR0", cp, T.VR0[:], T.OA[:, 256:512])
+        todo += equal(0, "Wf", lambda c: T.Wf[:, c:c + 1])
+        fill(0, 99)
+        if t < 2:
+            starts(t + 1)
+        view = lambda jp: RK[:, 4 - jp:8 - jp, 4 * jp - 4:4 * jp]
+        op("v", rk + " key%d" % t, "n1", tt, T.n1[:], view(1), view(2), A.max)
+        op("v", rk + " key%d" % t, "n2", tt, T.n2[:], view(3), view(4), A.max)
+        op("v", "n1 n2", "best", tt, T.best[:], T.n1[:], T.n2[:], A.max)
+        op("v", "best key%d" % t, "ON2", tt, T.ON[:, 32:48], T.best[:], key, A.not_equal)
+        op("v", "best", "c3", ts, T.c23[:, 0:16], T.best[:], 5 * 2048.0, None, A.is_lt)
+        op("v", "best", "c2", ts, T.c23[:, 16:32], T.best[:], 9 * 2048.0, None, A.is_lt)
+        op("v", "best key%d" % t, "eqw", tt, T.eqw[:], T.best[:], key, A.is_equal)
+        op("v", "best", "uI", ts, T.uI[:], T.best[:], 2047, None, A.bitwise_and)
+        op("v", "ON2 c3", "ON0", tt, T.ON[:, 0:16], T.ON[:, 32:48], T.c23[:, 0:16], A.mult)
+        op("v", "ON2 c2", "ON1", tt, T.ON[:, 16:32], T.ON[:, 32:48], T.c23[:, 16:32], A.mult)
+        op("v", "eqw wpos", "ON3", tt, T.ON[:, 48:64], T.eqw[:], T.wpos[:], A.mult)
+        on = "ON0 ON1 ON2 ON3"
+        for i in range(8):
+            o = T.onR[:, 64 * i:64 * i + 64]
+            if i % 2:
+                op("s", "gmask " + on, "onR%d" % i, act, o, T.ON[:], F.Copy, 0.0, T.gmask[:, i:i + 1])
+            else:
+                op("v", "gmask " + on, "onR%d" % i, ts, o, T.ON[:], T.gmask[:, i:i + 1], None, A.mult)
+        op("v", "uI expo dmask", "tmp", tt, T.tmp[:], T.uI[:].indirect(T.expo[:]), T.dmask[:], A.mult)
+
+        def place(o):
+            return ("#WL", T.WL[:, 16 * o:16 * o + 16]) if o % 2 == 0 else ("#D0", T.D0[:, o, 0:16])
+
+        def rivals(o, i):
+            bank = T.SC if o % 2 == 0 else T.ZD
+            b, c = "#SC" if o % 2 == 0 else "#ZD", "cD%d" % o
+            mm(" ".join("onR%d" % x for x in range(8)) + " E%d" % i, b, [(bank[0:8, 16 * q:256], T.onR[:, 16 * o + q:512:64], T["E%d" % i][:, q, 0:256 - 16 * q], q == 0, q == 15)
+                                  for q in range(16)])
+            op("s", b, c, act, T.cD[0:8, 256 * o:256 * o + 256], bank[0:8, 0:256], F.Copy)
+            if o == 0:
+                mm("B1 tmp", "#OA", [(T.OA[:, 256:512], T.B1[:], T.tmp[:], True, True)])
+            tag, out = place(o)
+            mm("Q8 " + c, tag, [(out, T.Q8[0:8, 128 * p:128 * p + 128], T.cD[0:8, 256 * o + p:256 * o + 256:16], p == 0, p == 15)
+                                for p in range(16)])
+
+        def offsets(o, tag, lst):
+            z = str(o)
+            at = lambda b: b[:, 16 * o:16 * o + 16]
+            tag2, got = place(o)
+            return [("v", tag2 + " ON" + z, "ns" + z, tt, at(T.ns), got, at(T.ON), A.is_ge),
+                    ("v", "spare ns" + z, "nd" + z, tt, at(T.nd), at(T.ns), T.spare[:], A.mult),
+                    ("v", "nd%s %s" % (z, tag), "of" + z, tt, at(T.of), at(T.nd), lst, A.max),
+                    ("v", "of" + z, "ou" + z, cp, at(T.ou), at(T.of))]
+
+        def factor(s):
+            op("v", "#OA OAs%d" % (s - 1), "Um%d" % s, tt, T.Um[:, s, :], T.OA[:, 256:512], T.OAs[:, 256 * s - 256:256 * s], A.mult)
+            op("s", "Um%d" % s, "Am%d" % s, act, T.Am[:, s, :], T.Um[:, s, :], F.Copy, 32.0)
+
+        def level(s, o, other):
+            z = str(s)
+            tag, lst = ("VLu%d" % t, T.VLu[:, 16 * t:16 * t + 16]) if s == 1 else ("WU%d0 WU%d1" % (s - 2, s - 2), T.WU[:, 16 * s - 32:16 * s - 16])
+            op("v", "K Am%s %s" % (z, tag), "pp" + z, tt, T.pp[:, s, :], Kwin.indirect(lst), T.Am[:, s, :], A.mult)
+            for x in other[0:1]:
+                op(*x)
+            op("v", "pp%s #D%s" % (z, z), "q" + z, tt, T.qq[:, s, :], T.pp[:, s, :], T["D" + z][:, 0:4, :], A.add)
+            for x in other[1:2]:
+                op(*x)
+            op("v", "q" + z, "r" + z, ts, T.rr[:, s, :], T.qq[:, s, :], 5, 2047, A.arith_shift_right, A.bitwise_and)
+            for x in other[2:3]:
+                op(*x)
+            op("v", "r%s ou%d" % (z, o), "K", cp, T.K[:].indirect(T.ou[:, 16 * o:16 * o + 16]), T.rr[:, s, :])
+            for x in other[3:]:
+                op(*x)
+        rivals(0, 3)
+        for s in (3, 2, 1):
+            factor(s)
+        rivals(1, 2)
+        for x in offsets(0, "wl1", T.wlf[:, 2:4, :]):
+            op(*x)
+        level(3, 0, offsets(1, "wl0", T.wlf[:, 4:6, :]))
+        rivals(3, 0)
+        rivals(2, 1)
+        level(2, 1, offsets(3, "Wf", T.Wf[:]))
+        last = offsets(2, "VL%d" % t, T.VL[:, 16 * t:16 * t + 16])
+        for x in last[:3]:
+            op(*x)
+        op("v", "nX ou3", "X", cp, T.X[:].indirect(T.ou[:, 48:64]), T.nX[:])
+        level(1, 2, last[3:])
+        if t < 2:
+            mm("ones ON3", "#ZD", [(T.ZD[:, 304:320], T.ones[:], T.ON[:, 48:64], True, True)])
+            op("v", "#ZD", "pr", V.tensor_reduce, T.pr[:], T.ZD[:, 304:320], AxisListType.X, A.add)
+            op("v", "pr", "pr2", cp, T.pr2[:, 0:1], T.pr[:])
+            op("v", "pr2", "pr3", ts, T.pr2[:, 1:2], T.pr2[:, 0:1], 1, None, A.bitwise_and)
+            op("v", "pr3", "thr", ts, T.thr[:], T.pr2[:, 1:2], 2.0, 8.0, A.mult, A.add)
+
+    for t in range(3):
+        race(t)
+
+    mm("WIb X", "#D0", [(T.D0[:, 0:4, :], T.WIb[:, 128 * a:128 * a + 128], T.X[:, 256 * a:256 * a + 256], a == 0, a == 7) for a in range(8)])
+    op("s", "#D0", "oX", act, T.oX[:], T.D0[:, 0:4, :], F.Copy)
+    dma("y", "sx", "oX", "", T.yx[:], T.oX[:])
+    op("v", "K", "KH0", cp, T.KH[:, 0:512], T.K[:, 0:512])
+    op("v", "K", "KH1", cp, T.KH[:, 512:1280], T.K[:, 512:1280])
+    mm("WIf K", "#D1", [(T.D1[:, 0:4, :], T.WIf[:, 128 * (a - 5):128 * (a - 4)], T.K[:, 256 * a:256 * a + 256], a == 5, False) for a in (5, 6, 7)])
+    mm("WIh KH0", "#D1", [(T.D1[:, 0:4, :], T.WIh[:, 128 * a:128 * a + 128], T.KH[:, 256 * a:256 * a + 256], False, False) for a in (0, 1)])
+    mm("WIh KH1", "#D1", [(T.D1[:, 0:4, :], T.WIh[:, 128 * a:128 * a + 128], T.KH[:, 256 * a:256 * a + 256], False, a == 4) for a in (2, 3, 4)])
+    op("v", "#D1", "oK", cp, T.oK[:], T.D1[:, 0:4, :])
+    dma("y", "sk", "oK", "", T.yk[:], T.oK[:])
+    for sem in sorted(cnt):
+        g.wait_ge(T.sem[sem], cnt[sem])

@@ -41,12 +41,15 @@ _sb(f32, oX=256, oK=256)
 _sb(h16, KH=1280)
 for _n in ("D0", "D1", "D2", "D3"):
     SCRATCH[_n] = ("psum", [128, 8, 64], f32)
-for _n in ("SC", "OA", "WL", "ZD"):
+for _n in ("SC", "OA", "ZD"):
     SCRATCH[_n] = ("psum", [128, 512], f32)
+SCRATCH["WL"] = ("psum", [128, 32, 16], f32)
 
 _LOADS = ["lz", "lv", "lx", "lk0", "lk1", "lk2", "lk3", "sx", "sk"]
-SEMAPHORES = ["qv", "qs", "qt", "qg", "zarr", "karr0", "karr1", "karr2", "sent"] + _LOADS
-FILL = (0, 3, 2, 0)
+SEMAPHORES = ["qv", "qs", "qt", "qg", "zarr0", "zarr1", "karr0", "karr1", "karr2", "sent"] + _LOADS
+ORDER = ("z2 KvU G T1a T1b f1 zs1 Gs sg zs0 scan sub0 C eq zs2 f0 kvf R0 OA PA sub1 OAs R1 sub2 WL f2 WR zs3 wl R2 vr wlf xw sum "
+         "sub3 f3 ZD R3").split()
+FILL = (0, 0, 3, 0)
 BIG = 8388608.0
 
 
@@ -141,10 +144,12 @@ def rank_program(g, core, T, topo):
     iota("dd", [[-1, 128]], 0, 1)
     iota("gm2", [[-16, 8]], 0, 1)
     iota("pint", [[0, 1]], 0, 1)
-    op("v", "z0s", "pk", cp, T.pk[:, 0:192], T.z0s[:])
-    op("v", "v0s", "pk", cp, T.pk[:, 192:240], T.v0s[:])
-    got = send("pk", "zarr", T.pk[:], [((rank + j) % n, T.ZL[:, 240 * (j - 1):240 * j]) for j in (1, 2, 3, 4)])
-    arrives("ZL", "zarr", got)
+    op("v", "z0s", "pk0", cp, T.pk[:, 0:64], T.z0s[:, 0:64])
+    op("v", "v0s", "pk0", cp, T.pk[:, 64:80], T.v0s[:, 0:16])
+    got = send("pk0", "zarr0", T.pk[:, 0:80], [((rank + j) % n, T.ZL[:, 80 * j - 80:80 * j]) for j in (1, 2, 3, 4)])
+    arrives("ZL0", "zarr0", got)
+    op("v", "z0s", "pk1", cp, T.pk[:, 80:208], T.z0s[:, 64:192])
+    op("v", "v0s", "pk1", cp, T.pk[:, 208:240], T.v0s[:, 16:48])
 
     iota("it16", [[0, 16], [1, 16]], 0, 0)
     iota("rst", [[0, 8], [1, 16]], 0, 0)
@@ -153,6 +158,8 @@ def rank_program(g, core, T, topo):
     iota("keyc", [[8192, 3], [-2048, 4], [0, 4]], 4 * 2048, 0)
     iota("zoffc", [[512, 3], [256, 2], [16, 8]], 128, 0)
     iota("spare", [[16, 16]], 2048, 0)
+    got = send("pk1", "zarr1", T.pk[:, 80:240], [((rank + j) % n, T.ZL[:, 160 + 160 * j:320 + 160 * j]) for j in (1, 2, 3, 4)])
+    arrives("ZL1", "zarr1", got)
     op("v", "dd", "I", ts, T.I[:], T.dd[:], 0.0, None, A.is_equal)
     op("v", "dd", "nI", ts, T.nI[:], T.dd[:], 0.0, -1.0, A.is_equal, A.mult)
     op("v", "gm2", "pc", ts, T.gmask[:], T.gm2[:], 0.0, None, A.is_ge)
@@ -181,10 +188,12 @@ def rank_program(g, core, T, topo):
         op("v", "K0%d" % b, "K", cp, T.K[:, 512 * b:512 * b + 512], T.K0[:, 512 * b:512 * b + 512])
 
     def starts(t):
+        zl = "ZL1" if t else "ZL0"
         for j in range(4):
-            op("v", "ZL", "zc%d" % t, cp, T.zc[:, 256 * t + 64 * j:256 * t + 64 * j + 64], T.ZL[:, 240 * j + 64 * t:240 * j + 64 * t + 64])
+            a, b = (320 + 160 * j + 64 * t - 64, 320 + 160 * j + 112 + 16 * t + 4 * j) if t else (80 * j, 80 * j + 64 + 4 * j)
             c = 16 * t + 4 * j
-            op("v", "ZL", "VL%d" % t, cp, T.VL[:, c:c + 4], T.ZL[:, 240 * j + 192 + c:240 * j + 192 + c + 4])
+            op("v", zl, "VL%d" % t, cp, T.VL[:, c:c + 4], T.ZL[:, b:b + 4])
+            op("v", zl, "zc%d" % t, cp, T.zc[:, 256 * t + 64 * j:256 * t + 64 * j + 64], T.ZL[:, a:a + 64])
         op("v", "VL%d" % t, "VLu%d" % t, cp, T.VLu[:, 16 * t:16 * t + 16], T.VL[:, 16 * t:16 * t + 16])
     starts(0)
 
@@ -211,14 +220,13 @@ def rank_program(g, core, T, topo):
         return ("VLu%d" % t, T.VLu[:, 16 * t + 8 * h:16 * t + 8 * h + w]) if s == 0 else \
             ("WU%d%d" % (s - 1, h), T.WU[:, 16 * (s - 1) + 8 * h:16 * (s - 1) + 8 * h + w])
 
+    def zpath0(t, s, h):
+        op("s", "X WU%d%d" % (s, h), "xw%d" % h, act, T["xw%d" % h][:], Xwin.indirect(T.WU[:, 16 * s + 8 * h:16 * s + 8 * h + 8]), F.Copy)
+
     def zpath1(t, s, h):
-        H = str(h)
         tag, zb, z0 = zat(t, s, h)
-        zz = zb[:, z0:z0 + 128]
-        w = "WU%d%d" % (s, h)
-        op("s", "X " + w, "xw" + H, act, T["xw" + H][:], Xwin.indirect(T.WU[:, 16 * s + 8 * h:16 * s + 8 * h + 8]), F.Copy)
-        xw = T["xw" + H][:]
-        mm("I nI chalf xw%s %s" % (H, tag), "#ZD", [
+        xw, zz = T["xw%d" % h][:], zb[:, z0:z0 + 128]
+        mm("I nI chalf xw%d %s" % (h, tag), "#ZD", [
             (T.ZD[:, 0:256], T.I[:], T.chalf[:], True, False), (T.ZD[:, 0:128], T.I[:], xw, False, False),
             (T.ZD[:, 128:256], T.I[:], xw, False, False), (T.ZD[:, 0:128], T.nI[:], zz, False, False),
             (T.ZD[:, 128:256], T.I[:], zz, False, True)])
@@ -236,22 +244,28 @@ def rank_program(g, core, T, topo):
     def sums(steps):
         tags = " ".join("z%d%d sg%d%d" % (s, h, s, h) for s in steps for h in (0, 1))
         a, b = slot(max(steps), 0), slot(min(steps), 1) + 256
-        w = (b - a) // 16
-        mm("Pb " + tags, "#ZD", [
-            (T.ZD[:, 256:256 + w], T.Pb[:, 128 * p:128 * p + 128], T.ZB[:, a + p:b:16], p == 0, p == 15) for p in range(16)])
-        op("s", "#ZD", "CLS%d" % len(steps), act, T.CLS[:, a // 256:b // 256, :], T.ZD[:, 256:256 + w], F.Copy)
+        mm("Pb " + tags, "#WL", [
+            (T.WL[:, 16 + a // 256:16 + b // 256, :], T.Pb[:, 128 * p:128 * p + 128], T.ZB[:, a + p:b:16], p == 0, p == 15) for p in range(16)])
 
-    def sub(t, s, h, b):
+    def keys(lo, hi):
+        at = lambda b: b[:, lo:hi, :]
+        z = str(lo)
+        op("v", "thr #WL", "bk" + z, ts, at(T.bk), T.WL[:, 16 + lo:16 + hi, 0:8], T.thr[:], None, A.is_ge)
+        op("v", "wl0 wl1 wl2 #WL", "us" + z, tt, at(T.us), at(T.wlf), T.WL[:, 16 + lo:16 + hi, 8:16], A.mult)
+        op("v", "us" + z, "ui" + z, ts, at(T.ui), at(T.us), 2047, None, A.bitwise_and)
+        op("v", "keyc ui" + z, "ks" + z, tt, at(T.ks), at(T.ui), at(T.keyc), A.add)
+        op("v", "ks%s bk%s" % (z, z), "kb" + z, tt, at(T.kb), at(T.ks), at(T.bk), A.mult)
+
+    def sub(t, s, h, b, first):
         H, ch, kh = str(h), b // 2, b % 2
         tag, zb, z0 = zat(t, s, h)
         zz = zb[:, z0 + 64 * ch:z0 + 64 * ch + 64]
-        D = T["D%d" % (2 * ch + kh)]
-        calls = []
-        for k8 in range(8):
-            k = 8 * kh + k8
-            calls.append((D[:, k8, :], T.I[:], T["XK" + H][:, 1024 * ch + k:1024 * (ch + 1):16], True, False))
-            calls.append((D[:, k8, :], T.nI[:], zz, False, True))
-        mm("I nI XK%s%d %s" % (H, ch, tag), "#D%d" % (2 * ch + kh), calls)
+        D = T["D%d" % b]
+        if first:
+            mm("nI " + tag, "#D%d" % b, [(D[:, k8, :], T.nI[:], zz, k8 == 0, False) for k8 in range(8)])
+        else:
+            mm("I XK%s%d" % (H, ch), "#D%d" % b, [
+                (D[:, k8, :], T.I[:], T["XK" + H][:, 1024 * ch + 8 * kh + k8:1024 * (ch + 1):16], False, k8 == 7) for k8 in range(8)])
 
     def relu(h, b):
         H, ch, kh = str(h), b // 2, b % 2
@@ -266,76 +280,67 @@ def rank_program(g, core, T, topo):
         op("s", "K " + tag, "KvF%d" % h, act, T["KvF%d" % h][:], Kwin.indirect(lst), F.Copy)
 
     def period(t, front, tail, fill):
+        todo = {}
         if front:
             s, h = front
             H = str(h)
             tag, lst = holders(t, s, h, 8)
-            op("v", "K " + tag, "KvU" + H, cp, T["KvU" + H][:], Kwin.indirect(lst))
+            todo["KvU"] = lambda: op("v", "K " + tag, "KvU" + H, cp, T["KvU" + H][:], Kwin.indirect(lst))
+            todo["G"] = lambda: op("v", "X KvU" + H, "XK%s0" % H, cp, T["XK" + H][:, 0:1024], Xwin.indirect(T["KvU" + H][:, 0:64]))
+            todo["Gs"] = lambda: op("s", "X KvU" + H, "XK%s1" % H, act, T["XK" + H][:, 1024:2048],
+                                    Xwin.indirect(T["KvU" + H][:, 64:128]), F.Copy)
+            if s:
+                todo["z2"] = lambda: zpath2(t, s - 1, h)
+                todo["sg"] = lambda: zpath3(t, s - 1, h)
+            todo["kvf"] = lambda: kvf(t, s, h)
+            for b in range(4):
+                todo["zs%d" % b] = lambda b=b: sub(t, s, h, b, True)
+                todo["sub%d" % b] = lambda b=b: sub(t, s, h, b, False)
+                todo["R%d" % b] = lambda b=b: relu(h, b)
+        else:
+            todo["z2"] = lambda: zpath2(t, 2, 0)
+            todo["sg"] = lambda: zpath3(t, 2, 0)
+            todo["sum"] = lambda: sums((0, 1))
         if tail:
             s2, h2 = tail
-            G = str(h2)
-            mm("ones order Sel " + " ".join("XM%s%d" % (G, b) for b in range(4)), "#SC",
-               [(T.SC[:, 0:128], T.ones[0:1, :], T.order[0:1, :], True, False)] +
-               [(T.SC[:, k:128:16], T["XM" + G][:, k, :], T.Sel[:], False, k == 15) for k in range(16)])
-        if front:
-            if s:
-                zpath2(t, s - 1, h)
-            op("v", "X KvU" + H, "XK%s0" % H, cp, T["XK" + H][:, 0:1024], Xwin.indirect(T["KvU" + H][:, 0:64]))
-            op("s", "X KvU" + H, "XK%s1" % H, act, T["XK" + H][:, 1024:2048], Xwin.indirect(T["KvU" + H][:, 64:128]), F.Copy)
-            if s:
-                zpath3(t, s - 1, h)
-            kvf(t, s, h)
-            sub(t, s, h, 0)
-        else:
-            zpath2(t, s2, 0)
-            zpath3(t, s2, 0)
-        if tail:
-            op("v", "rst #SC", "R" + G, V.tensor_tensor_scan, T["RC" + G][:, 0:128], T.rst[:], T.SC[:, 0:128], 0.0, A.mult, A.max)
-            op("v", "#SC", "C" + G, cp, T["RC" + G][:, 128:256], T.SC[:, 0:128])
-            op("v", "offK R%s C%s" % (G, G), "St" + G, tt, T["St" + G][:], T["RC" + G][:, 0:128].indirect(T.offK[:]),
-               T["RC" + G][:, 128:256], A.is_equal)
-            mm("I St" + G, "#OA", [(T.OA[:, 0:128], T["St" + G][:], T.I[:], True, True)])
-        fill(0)
-        if front:
-            sub(t, s, h, 1)
-            relu(h, 0)
-        fill(1)
-        if tail:
-            op("v", "#OA KvF" + G, "PA" + G, tt, T["PA" + G][:], T.OA[:, 0:128], T["KvF" + G][:], A.mult)
-            op("s", "#OA", "OAs%d" % s2, act, T.OAs[:, 256 * s2 + 128 * h2:256 * s2 + 128 * h2 + 128], T.OA[:, 0:128], F.Copy)
-            if front:
-                sub(t, s, h, 2)
-            mm("Pb PA" + G, "#WL", [
-                (T.WL[:, 0:8], T.Pb[:, 128 * p:128 * p + 128], T["PA" + G][:, p:128:16], p == 0, p == 15) for p in range(16)])
+            Y = str(h2)
+            RC, vr = T["RC" + Y], "VR%d" % (s2 + 2)
+            todo["T1a"] = lambda: mm(
+                "ones order Sel XM%s0 XM%s2" % (Y, Y), "#SC", [(T.SC[:, 0:128], T.ones[0:1, :], T.order[0:1, :], True, False)] +
+                [(T.SC[:, k:128:16], T["XM" + Y][:, k, :], T.Sel[:], False, False) for k in range(8)])
+            todo["T1b"] = lambda: mm(
+                "Sel XM%s1 XM%s3" % (Y, Y), "#SC", [(T.SC[:, k:128:16], T["XM" + Y][:, k, :], T.Sel[:], False, k == 15) for k in range(8, 16)])
+            todo["scan"] = lambda: op("v", "rst #SC", "R" + Y, V.tensor_tensor_scan, RC[:, 0:128], T.rst[:], T.SC[:, 0:128], 0.0, A.mult, A.max)
+            todo["C"] = lambda: op("v", "#SC", "C" + Y, cp, RC[:, 128:256], T.SC[:, 0:128])
+            todo["eq"] = lambda: op("v", "offK R%s C%s" % (Y, Y), "St" + Y, tt, T["St" + Y][:], RC[:, 0:128].indirect(T.offK[:]),
+                                    RC[:, 128:256], A.is_equal)
+            todo["OA"] = lambda: mm("I St" + Y, "#OA", [(T.OA[:, 0:128], T["St" + Y][:], T.I[:], True, True)])
+            todo["PA"] = lambda: op("v", "#OA KvF" + Y, "PA" + Y, tt, T["PA" + Y][:], T.OA[:, 0:128], T["KvF" + Y][:], A.mult)
+            todo["OAs"] = lambda: op("s", "#OA", "OAs%d" % s2, act, T.OAs[:, 256 * s2 + 128 * h2:256 * s2 + 128 * h2 + 128], T.OA[:, 0:128], F.Copy)
+            todo["WL"] = lambda: mm("Pb PA" + Y, "#WL", [
+                (T.WL[:, 0, 0:8], T.Pb[:, 128 * p:128 * p + 128], T["PA" + Y][:, p:128:16], p == 0, p == 15) for p in range(16)])
+            todo["wl"] = lambda: op("v", "#WL", "WU%d%d" % (s2, h2), cp, T.WU[:, 16 * s2 + 8 * h2:16 * s2 + 8 * h2 + 8], T.WL[:, 0, 0:8])
+            todo["wlf"] = lambda: op("s", "#WL", "wl%d" % s2, act, T.wlf[:, 4 - 2 * s2 + h2, :], T.WL[:, 0, 0:8], F.Copy)
+            todo["xw"] = lambda: zpath0(t, s2, h2)
+            todo["ZD"] = lambda: zpath1(t, s2, h2)
             if s2 < 2:
-                vr = "VR%d" % (s2 + 2)
-                mm("B1 PA" + G, "#OA", [(T.OA[:, 128:256], T.B1[:], T["PA" + G][:], True, True)])
-        if front:
-            relu(h, 1)
-            if not tail:
-                sub(t, s, h, 2)
-            relu(h, 2)
-            sub(t, s, h, 3)
-        else:
-            sums((0, 1))
-        fill(2)
-        if tail:
-            op("v", "#WL", "WU%d%d" % (s2, h2), cp, T.WU[:, 16 * s2 + 8 * h2:16 * s2 + 8 * h2 + 8], T.WL[:, 0:8])
-            zpath1(t, s2, h2)
-            op("s", "#WL", "wl%d" % s2, act, T.wlf[:, 4 - 2 * s2 + h2, :], T.WL[:, 0:8], F.Copy)
-            if s2 < 2:
-                op("v", "#OA", vr, cp, T[vr][:, 128 * h2:128 * h2 + 128], T.OA[:, 128:256])
-        if front:
-            relu(h, 3)
-        fill(3)
+                todo["WR"] = lambda: mm("B1 PA" + Y, "#OA", [(T.OA[:, 128:256], T.B1[:], T["PA" + Y][:], True, True)])
+                todo["vr"] = lambda: op("v", "#OA", vr, cp, T[vr][:, 128 * h2:128 * h2 + 128], T.OA[:, 128:256])
+        for k in range(4):
+            todo["f%d" % k] = lambda k=k: fill(k)
+        for name in ORDER:
+            if name in todo:
+                todo[name]()
 
     def spread(tag, lst):
         op("v", "dmask expo " + tag, "tmp", tt, T.tmp[:], lst.indirect(T.expo[:]), T.dmask[:], A.mult)
         mm("B1 tmp", "#OA", [(T.OA[:, 256:512], T.B1[:], T.tmp[:], True, True)])
 
-    def first(t):
-        spread("VL%d" % t, T.VL[:, 16 * t:16 * t + 16])
-        op("v", "#OA", "VR1", cp, T.VR1[:], T.OA[:, 256:512])
+    def first(t, k):
+        if k == 0:
+            spread("VL%d" % t, T.VL[:, 16 * t:16 * t + 16])
+        if k == 3:
+            op("v", "#OA", "VR1", cp, T.VR1[:], T.OA[:, 256:512])
 
     def equal(i, tag, col):
         e = T["E%d" % i]
@@ -353,7 +358,9 @@ def rank_program(g, core, T, topo):
         some = lambda k: fill(k, FILL[k])
         vlc = lambda c: T.VL[:, 16 * t + c:16 * t + c + 1]
         wc = lambda s: (lambda c: T.wlf[:, 4 - 2 * s + c // 8, c % 8:c % 8 + 1])
-        period(t, (0, 0), None, lambda k: k == 0 and first(t))
+        period(t, (0, 0), None, lambda k: first(t, k))
+        if t:
+            parity()
         todo += equal(1, "VL%d" % t, vlc)
         if t == 0:
             todo += late
@@ -364,28 +371,25 @@ def rank_program(g, core, T, topo):
         period(t, (2, 0), (1, 1), some)
         todo += equal(3, "wl1", wc(1))
         period(t, (2, 1), (2, 0), some)
-        period(t, None, (2, 1), lambda k: fill(k, (0, 4, 6, 0)[k]))
+        period(t, None, (2, 1), lambda k: fill(k, (0, 8, 6, 14)[k]))
+        keys(2, 6)
+        op("v", "kb2", "m1", tt, T.m1[:], T.kb[:, 2:4, :], T.kb[:, 4:6, :], A.max)
         zpath2(t, 2, 1)
         zpath3(t, 2, 1)
         sums((2,))
-        fill(0, 8)
-        cls = "CLS1 CLS2"
+        fill(0, 3)
         rk, RK = "RK%d" % t, T["RK%d" % t]
         key = RK[:, 3, :]
-        op("v", "thr " + cls, "bk", ts, T.bk[:], T.CLS[:, :, 0:8], T.thr[:], None, A.is_ge)
-        op("v", "wl0 wl1 wl2 " + cls, "us", tt, T.us[:], T.wlf[:], T.CLS[:, :, 8:16], A.mult)
-        op("v", "us", "ui", ts, T.ui[:], T.us[:], 2047, None, A.bitwise_and)
-        op("v", "ui keyc", "ks", tt, T.ks[:], T.ui[:], T.keyc[:], A.add)
-        op("v", "ks bk", "kb", tt, T.kb[:], T.ks[:], T.bk[:], A.mult)
-        op("v", "kb", "m1", tt, T.m1[:], T.kb[:, 0:2, :], T.kb[:, 2:4, :], A.max)
-        op("v", "kb m1", "key%d" % t, tt, key, T.m1[:], T.kb[:, 4:6, :], A.max)
+        keys(0, 2)
+        op("v", "kb0 m1", "key%d" % t, tt, key, T.m1[:], T.kb[:, 0:2, :], A.max)
+        bk = "bk0 bk2"
         got = send("key%d" % t, "karr%d" % t, key, [((rank - d) % n, RK[:, 3 - d, :]) for d in (-3, -2, -1, 1, 2, 3)])
         arrives(rk, "karr%d" % t, got)
         op("v", "key%d" % t, "wpos", ts, T.wpos[:], key, 0.5, None, A.is_ge)
-        op("v", "bk zoffc", "kz", tt, T.kz[:], T.zoffc[:], T.bk[:], A.mult)
+        op("v", "zoffc " + bk, "kz", tt, T.kz[:], T.zoffc[:], T.bk[:], A.mult)
         op("v", "keyc wl0 wl1 wl2", "kw", tt, T.kw[:], T.wlf[:], T.keyc[:], A.add)
         op("v", "kz", "kz2", tt, T.kz2[:], T.kz[:, 0:2, :], T.kz[:, 2:4, :], A.max)
-        op("v", "kw bk", "kw1", tt, T.kw1[:], T.kw[:], T.bk[:], A.mult)
+        op("v", "kw " + bk, "kw1", tt, T.kw1[:], T.kw[:], T.bk[:], A.mult)
         op("v", "kz kz2", "zo", tt, T.zo[:], T.kz2[:], T.kz[:, 4:6, :], A.max)
         op("v", "kw1", "kw2", tt, T.kw2[:], T.kw1[:, 0:2, :], T.kw1[:, 2:4, :], A.max)
         op("v", "zo", "zou", cp, T.zou[:], T.zo[:])
@@ -431,18 +435,23 @@ def rank_program(g, core, T, topo):
         op("v", "uI expo dmask", "tmp", tt, T.tmp[:], T.uI[:].indirect(T.expo[:]), T.dmask[:], A.mult)
 
         def place(o):
-            return ("#WL", T.WL[:, 16 * o:16 * o + 16]) if o % 2 == 0 else ("#D0", T.D0[:, o, 0:16])
+            return ("#WL", T.WL[:, o, :]) if o % 2 == 0 else ("#D0", T.D0[:, o, 0:16]) if o == 1 else ("#OA", T.OA[:, 0:16])
 
-        def rivals(o, i):
+        def rivals(o, i, between=None):
             bank = T.SC if o % 2 == 0 else T.ZD
             b, c = "#SC" if o % 2 == 0 else "#ZD", "cD%d" % o
-            mm(" ".join("onR%d" % x for x in range(8)) + " E%d" % i, b, [(bank[0:8, 16 * q:256], T.onR[:, 16 * o + q:512:64], T["E%d" % i][:, q, 0:256 - 16 * q], q == 0, q == 15)
-                                  for q in range(16)])
+            calls = [(bank[0:8, 16 * q:256], T.onR[:, 16 * o + q:512:64], T["E%d" % i][:, q, 0:256 - 16 * q], q == 0, q == 15) for q in range(16)]
+            on = " ".join("onR%d" % x for x in range(8)) + " E%d" % i
+            if between:
+                mm(on, b, calls[:4])
+                between()
+                calls = calls[4:]
+            mm(on, b, calls)
             op("s", b, c, act, T.cD[0:8, 256 * o:256 * o + 256], bank[0:8, 0:256], F.Copy)
-            if o == 0:
-                mm("B1 tmp", "#OA", [(T.OA[:, 256:512], T.B1[:], T.tmp[:], True, True)])
+
+        def listed(o):
             tag, out = place(o)
-            mm("Q8 " + c, tag, [(out, T.Q8[0:8, 128 * p:128 * p + 128], T.cD[0:8, 256 * o + p:256 * o + 256:16], p == 0, p == 15)
+            mm("Q8 cD%d" % o, tag, [(out, T.Q8[0:8, 128 * p:128 * p + 128], T.cD[0:8, 256 * o + p:256 * o + 256:16], p == 0, p == 15)
                                 for p in range(16)])
 
         def offsets(o, tag, lst):
@@ -458,42 +467,50 @@ def rank_program(g, core, T, topo):
             op("v", "#OA OAs%d" % (s - 1), "Um%d" % s, tt, T.Um[:, s, :], T.OA[:, 256:512], T.OAs[:, 256 * s - 256:256 * s], A.mult)
             op("s", "Um%d" % s, "Am%d" % s, act, T.Am[:, s, :], T.Um[:, s, :], F.Copy, 32.0)
 
-        def level(s, o, other):
+        def level(s, other):
             z = str(s)
             tag, lst = ("VLu%d" % t, T.VLu[:, 16 * t:16 * t + 16]) if s == 1 else ("WU%d0 WU%d1" % (s - 2, s - 2), T.WU[:, 16 * s - 32:16 * s - 16])
             op("v", "K Am%s %s" % (z, tag), "pp" + z, tt, T.pp[:, s, :], Kwin.indirect(lst), T.Am[:, s, :], A.mult)
-            for x in other[0:1]:
+            for x in other[0]:
                 op(*x)
             op("v", "pp%s #D%s" % (z, z), "q" + z, tt, T.qq[:, s, :], T.pp[:, s, :], T["D" + z][:, 0:4, :], A.add)
-            for x in other[1:2]:
+            for x in other[1]:
                 op(*x)
             op("v", "q" + z, "r" + z, ts, T.rr[:, s, :], T.qq[:, s, :], 5, 2047, A.arith_shift_right, A.bitwise_and)
-            for x in other[2:3]:
+            for x in other[2]:
                 op(*x)
-            op("v", "r%s ou%d" % (z, o), "K", cp, T.K[:].indirect(T.ou[:, 16 * o:16 * o + 16]), T.rr[:, s, :])
-            for x in other[3:]:
-                op(*x)
-        rivals(0, 3)
+
+        def write(s, o):
+            op("v", "r%d ou%d" % (s, o), "K", cp, T.K[:].indirect(T.ou[:, 16 * o:16 * o + 16]), T.rr[:, s, :])
+        rivals(0, 3, lambda: mm("B1 tmp", "#OA", [(T.OA[:, 256:512], T.B1[:], T.tmp[:], True, True)]))
+        listed(0)
         for s in (3, 2, 1):
             factor(s)
         rivals(1, 2)
+        rivals(3, 0)
+        listed(1)
+        rivals(2, 1)
+        listed(3)
+        level(3, ([], [], []))
         for x in offsets(0, "wl1", T.wlf[:, 2:4, :]):
             op(*x)
-        level(3, 0, offsets(1, "wl0", T.wlf[:, 4:6, :]))
-        rivals(3, 0)
-        rivals(2, 1)
-        level(2, 1, offsets(3, "Wf", T.Wf[:]))
-        last = offsets(2, "VL%d" % t, T.VL[:, 16 * t:16 * t + 16])
-        for x in last[:3]:
-            op(*x)
+        listed(2)
+        write(3, 0)
+        a = offsets(1, "wl0", T.wlf[:, 4:6, :])
+        level(2, (a[:1], a[1:2], a[2:]))
+        write(2, 1)
+        a, b = offsets(3, "Wf", T.Wf[:]), offsets(2, "VL%d" % t, T.VL[:, 16 * t:16 * t + 16])
+        level(1, (a[:1], [a[1], b[0]], [a[2], b[1], a[3], b[2]]))
         op("v", "nX ou3", "X", cp, T.X[:].indirect(T.ou[:, 48:64]), T.nX[:])
-        level(1, 2, last[3:])
-        if t < 2:
-            mm("ones ON3", "#ZD", [(T.ZD[:, 304:320], T.ones[:], T.ON[:, 48:64], True, True)])
-            op("v", "#ZD", "pr", V.tensor_reduce, T.pr[:], T.ZD[:, 304:320], AxisListType.X, A.add)
-            op("v", "pr", "pr2", cp, T.pr2[:, 0:1], T.pr[:])
-            op("v", "pr2", "pr3", ts, T.pr2[:, 1:2], T.pr2[:, 0:1], 1, None, A.bitwise_and)
-            op("v", "pr3", "thr", ts, T.thr[:], T.pr2[:, 1:2], 2.0, 8.0, A.mult, A.add)
+        op(*b[3])
+        write(1, 2)
+
+    def parity():
+        mm("ones ON3", "#ZD", [(T.ZD[:, 304:320], T.ones[:], T.ON[:, 48:64], True, True)])
+        op("v", "#ZD", "pr", V.tensor_reduce, T.pr[:], T.ZD[:, 304:320], AxisListType.X, A.add)
+        op("v", "pr", "pr2", cp, T.pr2[:, 0:1], T.pr[:])
+        op("v", "pr2", "pr3", ts, T.pr2[:, 1:2], T.pr2[:, 0:1], 1, None, A.bitwise_and)
+        op("v", "pr3", "thr", ts, T.thr[:], T.pr2[:, 1:2], 2.0, 8.0, A.mult, A.add)
 
     for t in range(3):
         race(t)

from concourse.bass import DstId, RemoteDMATransfer
from concourse.mybir import AluOpType as A, AxisListType, ActivationFunctionType as F

f32, b16, h16, i32, u16 = "float32", "bfloat16", "float16", "int32", "uint16"
SCRATCH = {}


def _sb(dtype, **shapes):
    for name, shape in shapes.items():
        SCRATCH[name] = ("sbuf", [128] + (list(shape) if isinstance(shape, (list, tuple)) else [shape]), dtype)


_sb(b16, X=2304, z0s=192, zc=768)
_sb(f32, K=2304, VL=48)
_sb(i32, K0=2048, v0s=48)
_sb(h16, pk=240, ZL=960)
_sb(u16, VLu=48, expo=16, offK=8)
_sb(f32, it16=256, itb=256, gmask=8, pcol=1, dd=128, dmask=256, rst=128, keyc=(6, 8), zoffc=(6, 8), spare=16, thr=1, gm2=8, WIf=384)
_sb(i32, pint=1, pr2=2)
_sb(b16, I=128, nI=128, ones=128, Sel=8, order=128, chalf=256, tri=(16, 16), Pb=2048, Q8=2048, Is=384, WIb=1024, B1=128)
_sb(h16, WIh=640)
for _h in "01":
    _sb(u16, **{"KvU" + _h: 128})
    _sb(f32, **{"KvF" + _h: 128, "RC" + _h: 256, "ZM" + _h: 128})
    _sb(b16, **{"XK" + _h: 2048, "XM" + _h: (16, 128), "St" + _h: 128, "xw" + _h: 128})
    _sb(h16, **{"PA" + _h: 128})
_sb(b16, OAs=768, ZB=1536)
_sb(u16, WU=48)
_sb(f32, wlf=(6, 8), CLS=(6, 16))
_sb(h16, VR0=256, VR1=256, VR2=256, VR3=256, tmp=256)
_sb(f32, bk=(6, 8), wpos=16, kz=(6, 8), kz2=(2, 8), zo=(2, 8), Wf=16, c23=32, eqw=16, pr=1, ZM2=256)
_sb(i32, us=(6, 8), ui=(6, 8), ks=(6, 8), kb=(6, 8), m1=(2, 8), kw=(6, 8), kw1=(6, 8), kw2=(2, 8), kw3=(2, 8), Wi=(2, 8), uI=16)
_sb(i32, RK0=(7, 16), RK1=(7, 16), RK2=(7, 16), n1=(4, 4), n2=(4, 4), best=(4, 4))
_sb(u16, zou=16, Wu=16)
_sb(b16, E0=(16, 256), E1=(16, 256), E2=(16, 256), E3=(16, 256), ON=64, onR=512, Zb=256, XWb=256, nX=256)
_sb(f32, Um=(4, 256), Am=(4, 256), pp=(4, 256), ns=64, nd=64, of=64)
_sb(i32, qq=(4, 256), rr=(4, 256))
_sb(b16, cD=1024)
_sb(u16, ou=64)
_sb(f32, oX=256, oK=256)
_sb(h16, KH=1280)
for _n in ("D0", "D1", "D2", "D3"):
    SCRATCH[_n] = ("psum", [128, 8, 64], f32)
for _n in ("SC", "OA", "ZD"):
    SCRATCH[_n] = ("psum", [128, 512], f32)
SCRATCH["WL"] = ("psum", [128, 32, 16], f32)

_LOADS = ["lz", "lv", "lx", "lk0", "lk1", "lk2", "lk3", "sx", "sk"]
SEMAPHORES = ["qv", "qs", "qt", "qg", "zarr0", "zarr1", "karr0", "karr1", "karr2", "sent"] + _LOADS
ORDER = ("z2 KvU G T1a T1b f1 zs1 Gs sg zs0 scan sub0 C eq zs2 f0 kvf R0 OA PA sub1 OAs R1 sub2 WL f2 WR zs3 wl R2 vr wlf xw sum "
         "sub3 f3 ZD R3").split()
FILL = (0, 0, 3, 0)
BIG = 8388608.0


def rank_program(g, core, T, topo):
    rank = T.rank_of(core)
    if rank is None:
        return
    n = len(T.cores)
    Q = {"v": g.vector, "s": g.scalar, "t": g.tensor, "g": g, "y": g.sync}
    V, S, P = Q["v"], Q["s"], Q["t"]
    cnt, snap, wr, rd = {}, {}, {}, {}
    know = {q: {} for q in Q}

    def deps(q, R, W):
        own, d = "q" + q, {}

        def want(table, t, same):
            for sem, val in table.get(t, {}).items():
                if same or sem != own:
                    d[sem] = max(d.get(sem, 0), val)
        for t in R:
            want(wr, t, True)
            if t[0] == "#":
                want(rd, t, False)
        for t in W:
            want(wr, t, False)
            want(rd, t, False)
        for sem in sorted(d, key=lambda x: (x == own, x)):
            val, k = d[sem], know[q]
            if k.get(sem, 0) >= val:
                continue
            Q[q].wait_ge(T.sem[sem], val)
            for s2, v2 in snap.get((sem, val), {}).items():
                k[s2] = max(k.get(s2, 0), v2)
            k[sem] = val

    def done(q, sem, inc, R, W):
        cnt[sem] = cnt.get(sem, 0) + inc
        snap[(sem, cnt[sem])] = dict(know[q])
        for t in R:
            rd.setdefault(t, {})[sem] = cnt[sem]
        for t in W:
            wr.setdefault(t, {})[sem] = cnt[sem]

    def op(q, R, W, f, *a, **k):
        R, W = R.split(), W.split()
        deps(q, R, W)
        f(*a, **k).then_inc(T.sem["q" + q], 1)
        done(q, "q" + q, 1, R, W)

    def mm(R, W, calls):
        R, W = R.split(), W.split()
        deps("t", R, W)
        for c in calls[:-1]:
            P.matmul(*c)
        P.matmul(*calls[-1]).then_inc(T.sem.qt, 1)
        done("t", "qt", 1, R, W)

    def dma(q, sem, R, W, out, in_):
        R, W = R.split(), W.split()
        deps(q, R, W)
        Q[q].dma_start(out, in_).then_inc(T.sem[sem], 16)
        done(q, sem, 16, R, W)

    def send(R, sem, src, dsts):
        deps("g", R.split(), [])
        ids, mask = [], topo.mask(core, T.cores[dsts[0][0]])
        for r, _ in dsts:
            rid, pid = topo.addr(T.cores[r], core)
            ids.append(DstId(rid=rid, pnc=pid))
            mask &= topo.mask(core, T.cores[r])
        g.remote_dma_fused([RemoteDMATransfer(dst_ids=ids, dma_engine_mask=mask, remote_sem=T.sem[sem], srcs=[src],
                                              dsts=[p for _, p in dsts])], local_sem=T.sem.sent)
        e = bin(mask).count("1")
        cnt["sent"] = cnt.get("sent", 0) + e
        return e * len(dsts)

    def arrives(tag, sem, val):
        cnt[sem] = val
        wr.setdefault(tag, {})[sem] = val

    ts, tt, cp, act = V.tensor_scalar, V.tensor_tensor, V.tensor_copy, S.activation

    dma("y", "lz", "", "z0s", T.z0s[:], T.z0[:])
    dma("y", "lv", "", "v0s", T.v0s[:], T.v0[:])
    for b in range(4):
        dma("y", "lk%d" % b, "", "K0%d" % b, T.K0[:, 512 * b:512 * b + 512], T.k0[:, 512 * b:512 * b + 512])
    dma("s", "lx", "", "X", T.X[:, 0:2048], T.x0[:])

    def iota(buf, pattern, base, cm):
        op("g", "", buf, g.iota, T[buf][:], pattern, base, cm, allow_small_or_imprecise_dtypes=True)
    iota("dd", [[-1, 128]], 0, 1)
    iota("gm2", [[-16, 8]], 0, 1)
    iota("pint", [[0, 1]], 0, 1)
    op("v", "z0s", "pk0", cp, T.pk[:, 0:64], T.z0s[:, 0:64])
    op("v", "v0s", "pk0", cp, T.pk[:, 64:80], T.v0s[:, 0:16])
    got = send("pk0", "zarr0", T.pk[:, 0:80], [((rank + j) % n, T.ZL[:, 80 * j - 80:80 * j]) for j in (1, 2, 3, 4)])
    arrives("ZL0", "zarr0", got)
    op("v", "z0s", "pk1", cp, T.pk[:, 80:208], T.z0s[:, 64:192])
    op("v", "v0s", "pk1", cp, T.pk[:, 208:240], T.v0s[:, 16:48])

    iota("it16", [[0, 16], [1, 16]], 0, 0)
    iota("rst", [[0, 8], [1, 16]], 0, 0)
    iota("order", [[0, 8], [-1, 16]], 15, 0)
    iota("itb", [[16, 16], [0, 16]], 0, 0)
    iota("keyc", [[8192, 3], [-2048, 4], [0, 4]], 4 * 2048, 0)
    iota("zoffc", [[512, 3], [256, 2], [16, 8]], 128, 0)
    iota("spare", [[16, 16]], 2048, 0)
    got = send("pk1", "zarr1", T.pk[:, 80:240], [((rank + j) % n, T.ZL[:, 160 + 160 * j:320 + 160 * j]) for j in (1, 2, 3, 4)])
    arrives("ZL1", "zarr1", got)
    op("v", "dd", "I", ts, T.I[:], T.dd[:], 0.0, None, A.is_equal)
    op("v", "dd", "nI", ts, T.nI[:], T.dd[:], 0.0, -1.0, A.is_equal, A.mult)
    op("v", "gm2", "pc", ts, T.gmask[:], T.gm2[:], 0.0, None, A.is_ge)
    op("v", "gm2", "gm2", ts, T.gm2[:], T.gm2[:], 16.0, None, A.is_lt)
    op("v", "gm2 pc", "gmask", tt, T.gmask[:], T.gmask[:], T.gm2[:], A.mult)
    op("v", "pint", "pint", ts, T.pint[:], T.pint[:], 15, None, A.bitwise_and)
    op("v", "pint", "pcol", cp, T.pcol[:], T.pint[:])
    op("v", "gmask", "Sel", ts, T.Sel[:], T.gmask[:], 16.0, None, A.mult)
    op("v", "", "ones", V.memset, T.ones[:], 1.0)
    op("v", "", "chalf", V.memset, T.chalf[:], -0.5)
    op("v", "", "thr", V.memset, T.thr[:], 8.0)
    op("v", "", "Pb", V.memset, T.Pb[:], 0.0)
    op("v", "", "B1", V.memset, T.B1[:], 0.0)
    op("v", "it16 pcol", "dmask", ts, T.dmask[:], T.it16[:], T.pcol[:], None, A.is_equal)
    op("v", "it16 pcol", "tri", ts, T.tri[:], T.it16[:], T.pcol[:], None, A.is_gt)
    op("v", "rst", "rst", ts, T.rst[:], T.rst[:], 0.0, None, A.is_gt)
    op("v", "it16", "expo", cp, T.expo[:], T.it16[:, 0:16])
    op("v", "itb", "offK", ts, T.offK[:], T.itb[:, 0:128:16], 15.0, None, A.add)
    op("v", "zoffc pcol", "zoffc", ts, T.zoffc[:], T.zoffc[:], T.pcol[:], None, A.add)
    op("v", "spare pcol", "spare", ts, T.spare[:], T.spare[:], T.pcol[:], None, A.add)
    for p in range(16):
        op("s", "gmask", "B1", act, T.B1[:, p:128:16], T.gmask[:], F.Copy)
        op("s", "gmask", "Pb", act, T.Pb[:, 128 * p + p:128 * (p + 1):16], T.gmask[:], F.Copy)

    for b in range(4):
        op("v", "K0%d" % b, "K", cp, T.K[:, 512 * b:512 * b + 512], T.K0[:, 512 * b:512 * b + 512])

    def starts(t):
        zl = "ZL1" if t else "ZL0"
        for j in range(4):
            a, b = (320 + 160 * j + 64 * t - 64, 320 + 160 * j + 112 + 16 * t + 4 * j) if t else (80 * j, 80 * j + 64 + 4 * j)
            c = 16 * t + 4 * j
            op("v", zl, "VL%d" % t, cp, T.VL[:, c:c + 4], T.ZL[:, b:b + 4])
            op("v", zl, "zc%d" % t, cp, T.zc[:, 256 * t + 64 * j:256 * t + 64 * j + 64], T.ZL[:, a:a + 64])
        op("v", "VL%d" % t, "VLu%d" % t, cp, T.VLu[:, 16 * t:16 * t + 16], T.VL[:, 16 * t:16 * t + 16])
    starts(0)

    late = [("v", "", "Q8", V.memset, T.Q8[0:8, :], 1.0),
            ("g", "Q8", "Q8", g.affine_select, T.Q8[0:8, :], T.Q8[0:8, :], [[-1, 16], [1, 128]], A.is_equal, 0.0, 0, -16)]
    for s in (1, 2, 3):
        late.append(("s", "I", "Is", act, T.Is[:, 128 * s - 128:128 * s], T.I[:], F.Copy, 0.0, 32.0 * s))
    for a in range(8):
        late.append(("s", "I", "WIb", act, T.WIb[:, 128 * a:128 * a + 128], T.I[:], F.Copy, 0.0, a + 1.0))
        if a < 5:
            late.append(("v", "I", "WIh", ts, T.WIh[:, 128 * a:128 * a + 128], T.I[:], a + 1.0, None, A.mult))
        else:
            late.append(("s", "I", "WIf", act, T.WIf[:, 128 * (a - 5):128 * (a - 4)], T.I[:], F.Copy, 0.0, a + 1.0))

    Kwin, Xwin = T.K[:, 0:2048], T.X[:, 0:2048]

    def slot(s, h):
        return ((2 - s) * 2 + h) * 256

    def zat(t, s, h):
        return ("zc%d" % t, T.zc, 256 * t + 128 * h) if s == 0 else ("z%d%d" % (s - 1, h), T.ZB, slot(s - 1, h) + 128)

    def holders(t, s, h, w):
        return ("VLu%d" % t, T.VLu[:, 16 * t + 8 * h:16 * t + 8 * h + w]) if s == 0 else \
            ("WU%d%d" % (s - 1, h), T.WU[:, 16 * (s - 1) + 8 * h:16 * (s - 1) + 8 * h + w])

    def zpath0(t, s, h):
        op("s", "X WU%d%d" % (s, h), "xw%d" % h, act, T["xw%d" % h][:], Xwin.indirect(T.WU[:, 16 * s + 8 * h:16 * s + 8 * h + 8]), F.Copy)

    def zpath1(t, s, h):
        tag, zb, z0 = zat(t, s, h)
        xw, zz = T["xw%d" % h][:], zb[:, z0:z0 + 128]
        mm("I nI chalf xw%d %s" % (h, tag), "#ZD", [
            (T.ZD[:, 0:256], T.I[:], T.chalf[:], True, False), (T.ZD[:, 0:128], T.I[:], xw, False, False),
            (T.ZD[:, 128:256], T.I[:], xw, False, False), (T.ZD[:, 0:128], T.nI[:], zz, False, False),
            (T.ZD[:, 128:256], T.I[:], zz, False, True)])

    def zpath2(t, s, h):
        H = str(h)
        op("s", "#ZD", "ZM" + H, act, T["ZM" + H][:], T.ZD[:, 128:256], F.Identity, BIG, 0.5)
        o = slot(s, h)
        op("s", "ZM" + H, "z%d%d" % (s, h), act, T.ZB[:, o + 128:o + 256], T["ZM" + H][:], F.Identity, -BIG)

    def zpath3(t, s, h):
        o = slot(s, h)
        op("s", "#ZD", "sg%d%d" % (s, h), act, T.ZB[:, o:o + 128], T.ZD[:, 0:128], F.Sign)

    def sums(steps):
        tags = " ".join("z%d%d sg%d%d" % (s, h, s, h) for s in steps for h in (0, 1))
        a, b = slot(max(steps), 0), slot(min(steps), 1) + 256
        mm("Pb " + tags, "#WL", [
            (T.WL[:, 16 + a // 256:16 + b // 256, :], T.Pb[:, 128 * p:128 * p + 128], T.ZB[:, a + p:b:16], p == 0, p == 15) for p in range(16)])

    def keys(lo, hi):
        at = lambda b: b[:, lo:hi, :]
        z = str(lo)
        op("v", "thr #WL", "bk" + z, ts, at(T.bk), T.WL[:, 16 + lo:16 + hi, 0:8], T.thr[:], None, A.is_ge)
        op("v", "wl0 wl1 wl2 #WL", "us" + z, tt, at(T.us), at(T.wlf), T.WL[:, 16 + lo:16 + hi, 8:16], A.mult)
        op("v", "us" + z, "ui" + z, ts, at(T.ui), at(T.us), 2047, None, A.bitwise_and)
        op("v", "keyc ui" + z, "ks" + z, tt, at(T.ks), at(T.ui), at(T.keyc), A.add)
        op("v", "ks%s bk%s" % (z, z), "kb" + z, tt, at(T.kb), at(T.ks), at(T.bk), A.mult)

    def sub(t, s, h, b, first):
        H, ch, kh = str(h), b // 2, b % 2
        tag, zb, z0 = zat(t, s, h)
        zz = zb[:, z0 + 64 * ch:z0 + 64 * ch + 64]
        D = T["D%d" % b]
        if first:
            mm("nI " + tag, "#D%d" % b, [(D[:, k8, :], T.nI[:], zz, k8 == 0, False) for k8 in range(8)])
        else:
            mm("I XK%s%d" % (H, ch), "#D%d" % b, [
                (D[:, k8, :], T.I[:], T["XK" + H][:, 1024 * ch + 8 * kh + k8:1024 * (ch + 1):16], False, k8 == 7) for k8 in range(8)])

    def relu(h, b):
        H, ch, kh = str(h), b // 2, b % 2
        out = T["XM" + H][:, 8 * kh:8 * kh + 8, 64 * ch:64 * ch + 64]
        if ch == 0:
            op("v", "#D%d" % b, "XM%s%d" % (H, b), ts, out, T["D%d" % b][:], 0.0, None, A.max)
        else:
            op("s", "#D%d" % b, "XM%s%d" % (H, b), act, out, T["D%d" % b][:], F.Relu)

    def kvf(t, s, h):
        tag, lst = holders(t, s, h, 8)
        op("s", "K " + tag, "KvF%d" % h, act, T["KvF%d" % h][:], Kwin.indirect(lst), F.Copy)

    def period(t, front, tail, fill):
        todo = {}
        if front:
            s, h = front
            H = str(h)
            tag, lst = holders(t, s, h, 8)
            todo["KvU"] = lambda: op("v", "K " + tag, "KvU" + H, cp, T["KvU" + H][:], Kwin.indirect(lst))
            todo["G"] = lambda: op("v", "X KvU" + H, "XK%s0" % H, cp, T["XK" + H][:, 0:1024], Xwin.indirect(T["KvU" + H][:, 0:64]))
            todo["Gs"] = lambda: op("s", "X KvU" + H, "XK%s1" % H, act, T["XK" + H][:, 1024:2048],
                                    Xwin.indirect(T["KvU" + H][:, 64:128]), F.Copy)
            if s:
                todo["z2"] = lambda: zpath2(t, s - 1, h)
                todo["sg"] = lambda: zpath3(t, s - 1, h)
            todo["kvf"] = lambda: kvf(t, s, h)
            for b in range(4):
                todo["zs%d" % b] = lambda b=b: sub(t, s, h, b, True)
                todo["sub%d" % b] = lambda b=b: sub(t, s, h, b, False)
                todo["R%d" % b] = lambda b=b: relu(h, b)
        else:
            todo["z2"] = lambda: zpath2(t, 2, 0)
            todo["sg"] = lambda: zpath3(t, 2, 0)
            todo["sum"] = lambda: sums((0, 1))
        if tail:
            s2, h2 = tail
            Y = str(h2)
            RC, vr = T["RC" + Y], "VR%d" % (s2 + 2)
            todo["T1a"] = lambda: mm(
                "ones order Sel XM%s0 XM%s2" % (Y, Y), "#SC", [(T.SC[:, 0:128], T.ones[0:1, :], T.order[0:1, :], True, False)] +
                [(T.SC[:, k:128:16], T["XM" + Y][:, k, :], T.Sel[:], False, False) for k in range(8)])
            todo["T1b"] = lambda: mm(
                "Sel XM%s1 XM%s3" % (Y, Y), "#SC", [(T.SC[:, k:128:16], T["XM" + Y][:, k, :], T.Sel[:], False, k == 15) for k in range(8, 16)])
            todo["scan"] = lambda: op("v", "rst #SC", "R" + Y, V.tensor_tensor_scan, RC[:, 0:128], T.rst[:], T.SC[:, 0:128], 0.0, A.mult, A.max)
            todo["C"] = lambda: op("v", "#SC", "C" + Y, cp, RC[:, 128:256], T.SC[:, 0:128])
            todo["eq"] = lambda: op("v", "offK R%s C%s" % (Y, Y), "St" + Y, tt, T["St" + Y][:], RC[:, 0:128].indirect(T.offK[:]),
                                    RC[:, 128:256], A.is_equal)
            todo["OA"] = lambda: mm("I St" + Y, "#OA", [(T.OA[:, 0:128], T["St" + Y][:], T.I[:], True, True)])
            todo["PA"] = lambda: op("v", "#OA KvF" + Y, "PA" + Y, tt, T["PA" + Y][:], T.OA[:, 0:128], T["KvF" + Y][:], A.mult)
            todo["OAs"] = lambda: op("s", "#OA", "OAs%d" % s2, act, T.OAs[:, 256 * s2 + 128 * h2:256 * s2 + 128 * h2 + 128], T.OA[:, 0:128], F.Copy)
            todo["WL"] = lambda: mm("Pb PA" + Y, "#WL", [
                (T.WL[:, 0, 0:8], T.Pb[:, 128 * p:128 * p + 128], T["PA" + Y][:, p:128:16], p == 0, p == 15) for p in range(16)])
            todo["wl"] = lambda: op("v", "#WL", "WU%d%d" % (s2, h2), cp, T.WU[:, 16 * s2 + 8 * h2:16 * s2 + 8 * h2 + 8], T.WL[:, 0, 0:8])
            todo["wlf"] = lambda: op("s", "#WL", "wl%d" % s2, act, T.wlf[:, 4 - 2 * s2 + h2, :], T.WL[:, 0, 0:8], F.Copy)
            todo["xw"] = lambda: zpath0(t, s2, h2)
            todo["ZD"] = lambda: zpath1(t, s2, h2)
            if s2 < 2:
                todo["WR"] = lambda: mm("B1 PA" + Y, "#OA", [(T.OA[:, 128:256], T.B1[:], T["PA" + Y][:], True, True)])
                todo["vr"] = lambda: op("v", "#OA", vr, cp, T[vr][:, 128 * h2:128 * h2 + 128], T.OA[:, 128:256])
        for k in range(4):
            todo["f%d" % k] = lambda k=k: fill(k)
        for name in ORDER:
            if name in todo:
                todo[name]()

    def spread(tag, lst):
        op("v", "dmask expo " + tag, "tmp", tt, T.tmp[:], lst.indirect(T.expo[:]), T.dmask[:], A.mult)
        mm("B1 tmp", "#OA", [(T.OA[:, 256:512], T.B1[:], T.tmp[:], True, True)])

    def first(t, k):
        if k == 0:
            spread("VL%d" % t, T.VL[:, 16 * t:16 * t + 16])
        if k == 3:
            op("v", "#OA", "VR1", cp, T.VR1[:], T.OA[:, 256:512])

    def equal(i, tag, col):
        e = T["E%d" % i]
        todo = [("v", "VR%d %s" % (i, tag), "E%d" % i, ts, e[:, c, 0:256 - 16 * c], T["VR%d" % i][:, 16 * c:256], col(c), None, A.is_equal)
                for c in range(16)]
        todo.append(("v", "tri E%d" % i, "E%d" % i, tt, e[:, :, 0:16], e[:, :, 0:16], T.tri[:], A.mult))
        return todo

    def race(t):
        todo = []

        def fill(k, lots=0):
            for _ in range(min(len(todo), lots)):
                op(*todo.pop(0))
        some = lambda k: fill(k, FILL[k])
        vlc = lambda c: T.VL[:, 16 * t + c:16 * t + c + 1]
        wc = lambda s: (lambda c: T.wlf[:, 4 - 2 * s + c // 8, c % 8:c % 8 + 1])
        period(t, (0, 0), None, lambda k: first(t, k))
        if t:
            parity()
        todo += equal(1, "VL%d" % t, vlc)
        if t == 0:
            todo += late
        period(t, (0, 1), (0, 0), some)
        period(t, (1, 0), (0, 1), some)
        todo += equal(2, "wl0", wc(0))
        period(t, (1, 1), (1, 0), some)
        period(t, (2, 0), (1, 1), some)
        todo += equal(3, "wl1", wc(1))
        period(t, (2, 1), (2, 0), some)
        period(t, None, (2, 1), lambda k: fill(k, (0, 8, 6, 14)[k]))
        keys(2, 6)
        op("v", "kb2", "m1", tt, T.m1[:], T.kb[:, 2:4, :], T.kb[:, 4:6, :], A.max)
        zpath2(t, 2, 1)
        zpath3(t, 2, 1)
        sums((2,))
        fill(0, 3)
        rk, RK = "RK%d" % t, T["RK%d" % t]
        key = RK[:, 3, :]
        keys(0, 2)
        op("v", "kb0 m1", "key%d" % t, tt, key, T.m1[:], T.kb[:, 0:2, :], A.max)
        bk = "bk0 bk2"
        got = send("key%d" % t, "karr%d" % t, key, [((rank - d) % n, RK[:, 3 - d, :]) for d in (-3, -2, -1, 1, 2, 3)])
        arrives(rk, "karr%d" % t, got)
        op("v", "key%d" % t, "wpos", ts, T.wpos[:], key, 0.5, None, A.is_ge)
        op("v", "zoffc " + bk, "kz", tt, T.kz[:], T.zoffc[:], T.bk[:], A.mult)
        op("v", "keyc wl0 wl1 wl2", "kw", tt, T.kw[:], T.wlf[:], T.keyc[:], A.add)
        op("v", "kz", "kz2", tt, T.kz2[:], T.kz[:, 0:2, :], T.kz[:, 2:4, :], A.max)
        op("v", "kw " + bk, "kw1", tt, T.kw1[:], T.kw[:], T.bk[:], A.mult)
        op("v", "kz kz2", "zo", tt, T.zo[:], T.kz2[:], T.kz[:, 4:6, :], A.max)
        op("v", "kw1", "kw2", tt, T.kw2[:], T.kw1[:, 0:2, :], T.kw1[:, 2:4, :], A.max)
        op("v", "zo", "zou", cp, T.zou[:], T.zo[:])
        op("v", "kw1 kw2", "kw3", tt, T.kw3[:], T.kw2[:], T.kw1[:, 4:6, :], A.max)
        op("v", "kw3", "Wi", ts, T.Wi[:], T.kw3[:], 2047, None, A.bitwise_and)
        op("v", "Wi", "Wf", cp, T.Wf[:], T.Wi[:])
        op("v", "Wi", "Wu", cp, T.Wu[:], T.Wi[:])
        spread("Wf", T.Wf[:])
        zb = " ".join("z%d%d sg%d%d" % (s, h, s, h) for s in range(3) for h in range(2))
        op("s", "zou " + zb, "Zb", act, T.Zb[:], T.ZB[:].indirect(T.zou[:]), F.Copy)
        op("s", "X Wu", "XWb", act, T.XWb[:], Xwin.indirect(T.Wu[:]), F.Copy)
        mm("I chalf Zb XWb", "#ZD", [(T.ZD[:, 0:256], T.I[:], T.chalf[:], True, False), (T.ZD[:, 0:256], T.I[:], T.Zb[:], False, False),
                                     (T.ZD[:, 0:256], T.I[:], T.XWb[:], False, True)])
        op("s", "#ZD", "ZM2", act, T.ZM2[:], T.ZD[:, 0:256], F.Identity, BIG, 0.5)
        op("s", "ZM2", "nX", act, T.nX[:], T.ZM2[:], F.Identity, -BIG)
        for s in (1, 2, 3):
            mm("Is OAs%d" % (s - 1), "#D%d" % s, [(T["D%d" % s][:, 0:4, :], T.Is[:, 128 * s - 128:128 * s], T.OAs[:, 256 * s - 256:256 * s], True, True)])
        fill(0, 99)
        op("v", "#OA", "VR0", cp, T.VR0[:], T.OA[:, 256:512])
        todo += equal(0, "Wf", lambda c: T.Wf[:, c:c + 1])
        fill(0, 99)
        if t < 2:
            starts(t + 1)
        view = lambda jp: RK[:, 4 - jp:8 - jp, 4 * jp - 4:4 * jp]
        op("v", rk + " key%d" % t, "n1", tt, T.n1[:], view(1), view(2), A.max)
        op("v", rk + " key%d" % t, "n2", tt, T.n2[:], view(3), view(4), A.max)
        op("v", "n1 n2", "best", tt, T.best[:], T.n1[:], T.n2[:], A.max)
        op("v", "best key%d" % t, "ON2", tt, T.ON[:, 32:48], T.best[:], key, A.not_equal)
        op("v", "best", "c3", ts, T.c23[:, 0:16], T.best[:], 5 * 2048.0, None, A.is_lt)
        op("v", "best", "c2", ts, T.c23[:, 16:32], T.best[:], 9 * 2048.0, None, A.is_lt)
        op("v", "best key%d" % t, "eqw", tt, T.eqw[:], T.best[:], key, A.is_equal)
        op("v", "best", "uI", ts, T.uI[:], T.best[:], 2047, None, A.bitwise_and)
        op("v", "ON2 c3", "ON0", tt, T.ON[:, 0:16], T.ON[:, 32:48], T.c23[:, 0:16], A.mult)
        op("v", "ON2 c2", "ON1", tt, T.ON[:, 16:32], T.ON[:, 32:48], T.c23[:, 16:32], A.mult)
        op("v", "eqw wpos", "ON3", tt, T.ON[:, 48:64], T.eqw[:], T.wpos[:], A.mult)
        on = "ON0 ON1 ON2 ON3"
        for i in range(8):
            o = T.onR[:, 64 * i:64 * i + 64]
            if i % 2:
                op("s", "gmask " + on, "onR%d" % i, act, o, T.ON[:], F.Copy, 0.0, T.gmask[:, i:i + 1])
            else:
                op("v", "gmask " + on, "onR%d" % i, ts, o, T.ON[:], T.gmask[:, i:i + 1], None, A.mult)
        op("v", "uI expo dmask", "tmp", tt, T.tmp[:], T.uI[:].indirect(T.expo[:]), T.dmask[:], A.mult)

        def place(o):
            return ("#WL", T.WL[:, o, :]) if o % 2 == 0 else ("#D0", T.D0[:, o, 0:16]) if o == 1 else ("#OA", T.OA[:, 0:16])

        def rivals(o, i, between=None):
            bank = T.SC if o % 2 == 0 else T.ZD
            b, c = "#SC" if o % 2 == 0 else "#ZD", "cD%d" % o
            calls = [(bank[0:8, 16 * q:256], T.onR[:, 16 * o + q:512:64], T["E%d" % i][:, q, 0:256 - 16 * q], q == 0, q == 15) for q in range(16)]
            on = " ".join("onR%d" % x for x in range(8)) + " E%d" % i
            if between:
                mm(on, b, calls[:4])
                between()
                calls = calls[4:]
            mm(on, b, calls)
            op("s", b, c, act, T.cD[0:8, 256 * o:256 * o + 256], bank[0:8, 0:256], F.Copy)

        def listed(o):
            tag, out = place(o)
            mm("Q8 cD%d" % o, tag, [(out, T.Q8[0:8, 128 * p:128 * p + 128], T.cD[0:8, 256 * o + p:256 * o + 256:16], p == 0, p == 15)
                                for p in range(16)])

        def offsets(o, tag, lst):
            z = str(o)
            at = lambda b: b[:, 16 * o:16 * o + 16]
            tag2, got = place(o)
            return [("v", tag2 + " ON" + z, "ns" + z, tt, at(T.ns), got, at(T.ON), A.is_ge),
                    ("v", "spare ns" + z, "nd" + z, tt, at(T.nd), at(T.ns), T.spare[:], A.mult),
                    ("v", "nd%s %s" % (z, tag), "of" + z, tt, at(T.of), at(T.nd), lst, A.max),
                    ("v", "of" + z, "ou" + z, cp, at(T.ou), at(T.of))]

        def factor(s):
            op("v", "#OA OAs%d" % (s - 1), "Um%d" % s, tt, T.Um[:, s, :], T.OA[:, 256:512], T.OAs[:, 256 * s - 256:256 * s], A.mult)
            op("s", "Um%d" % s, "Am%d" % s, act, T.Am[:, s, :], T.Um[:, s, :], F.Copy, 32.0)

        def level(s, other):
            z = str(s)
            tag, lst = ("VLu%d" % t, T.VLu[:, 16 * t:16 * t + 16]) if s == 1 else ("WU%d0 WU%d1" % (s - 2, s - 2), T.WU[:, 16 * s - 32:16 * s - 16])
            op("v", "K Am%s %s" % (z, tag), "pp" + z, tt, T.pp[:, s, :], Kwin.indirect(lst), T.Am[:, s, :], A.mult)
            for x in other[0]:
                op(*x)
            op("v", "pp%s #D%s" % (z, z), "q" + z, tt, T.qq[:, s, :], T.pp[:, s, :], T["D" + z][:, 0:4, :], A.add)
            for x in other[1]:
                op(*x)
            op("v", "q" + z, "r" + z, ts, T.rr[:, s, :], T.qq[:, s, :], 5, 2047, A.arith_shift_right, A.bitwise_and)
            for x in other[2]:
                op(*x)

        def write(s, o):
            op("v", "r%d ou%d" % (s, o), "K", cp, T.K[:].indirect(T.ou[:, 16 * o:16 * o + 16]), T.rr[:, s, :])
        rivals(0, 3, lambda: mm("B1 tmp", "#OA", [(T.OA[:, 256:512], T.B1[:], T.tmp[:], True, True)]))
        listed(0)
        for s in (3, 2, 1):
            factor(s)
        rivals(1, 2)
        rivals(3, 0)
        listed(1)
        rivals(2, 1)
        listed(3)
        level(3, ([], [], []))
        for x in offsets(0, "wl1", T.wlf[:, 2:4, :]):
            op(*x)
        listed(2)
        write(3, 0)
        a = offsets(1, "wl0", T.wlf[:, 4:6, :])
        level(2, (a[:1], a[1:2], a[2:]))
        write(2, 1)
        a, b = offsets(3, "Wf", T.Wf[:]), offsets(2, "VL%d" % t, T.VL[:, 16 * t:16 * t + 16])
        level(1, (a[:1], [a[1], b[0]], [a[2], b[1], a[3], b[2]]))
        op("v", "nX ou3", "X", cp, T.X[:].indirect(T.ou[:, 48:64]), T.nX[:])
        op(*b[3])
        write(1, 2)

    def parity():
        mm("ones ON3", "#ZD", [(T.ZD[:, 304:320], T.ones[:], T.ON[:, 48:64], True, True)])
        op("v", "#ZD", "pr", V.tensor_reduce, T.pr[:], T.ZD[:, 304:320], AxisListType.X, A.add)
        op("v", "pr", "pr2", cp, T.pr2[:, 0:1], T.pr[:])
        op("v", "pr2", "pr3", ts, T.pr2[:, 1:2], T.pr2[:, 0:1], 1, None, A.bitwise_and)
        op("v", "pr3", "thr", ts, T.thr[:], T.pr2[:, 1:2], 2.0, 8.0, A.mult, A.add)

    for t in range(3):
        race(t)

    mm("WIb X", "#D0", [(T.D0[:, 0:4, :], T.WIb[:, 128 * a:128 * a + 128], T.X[:, 256 * a:256 * a + 256], a == 0, a == 7) for a in range(8)])
    op("s", "#D0", "oX", act, T.oX[:], T.D0[:, 0:4, :], F.Copy)
    dma("y", "sx", "oX", "", T.yx[:], T.oX[:])
    op("v", "K", "KH0", cp, T.KH[:, 0:512], T.K[:, 0:512])
    op("v", "K", "KH1", cp, T.KH[:, 512:1280], T.K[:, 512:1280])
    mm("WIf K", "#D1", [(T.D1[:, 0:4, :], T.WIf[:, 128 * (a - 5):128 * (a - 4)], T.K[:, 256 * a:256 * a + 256], a == 5, False) for a in (5, 6, 7)])
    mm("WIh KH0", "#D1", [(T.D1[:, 0:4, :], T.WIh[:, 128 * a:128 * a + 128], T.KH[:, 256 * a:256 * a + 256], False, False) for a in (0, 1)])
    mm("WIh KH1", "#D1", [(T.D1[:, 0:4, :], T.WIh[:, 128 * a:128 * a + 128], T.KH[:, 256 * a:256 * a + 256], False, a == 4) for a in (2, 3, 4)])
    op("v", "#D1", "oK", cp, T.oK[:], T.D1[:, 0:4, :])
    dma("y", "sk", "oK", "", T.yk[:], T.oK[:])
    for sem in sorted(cnt):
        g.wait_ge(T.sem[sem], cnt[sem])
